import numpy as np, ml_dtypes
CORES = [48,51,52,55]
N = 4
import mx_ref
BF = ml_dtypes.bfloat16
def cols(t, e):
    v = np.concatenate([t.reshape(128, -1, 4), np.zeros((128, 1, 4), BF)], axis=1)
    return np.ascontiguousarray(v[:, e]).reshape(128, -1)
def cut(t, i, w=512):
    return t[:, w * i:w * i + w]
def pick(q, e):
    c = np.concatenate([q[0].reshape(128, -1, 4), np.zeros((128, 1, 4), np.uint8)], axis=1); s = np.concatenate([q[1], np.ones((16, 1), np.uint8)], axis=1)
    return (np.ascontiguousarray(c[:, e].reshape(128, -1)), np.ascontiguousarray(s[:, e]))
def join(*qs):
    return (np.concatenate([q[0] for q in qs], axis=1), np.concatenate([q[1] for q in qs], axis=1))
def put(q, e, v):
    c, s = q[0].reshape(128, -1, 4).copy(), q[1].copy(); c[:, e] = v[0].reshape(128, -1, 4); s[:, e] = v[1]
    return (c.reshape(128, -1), s)
def pk(c, s):
    return (np.ascontiguousarray(c), mx_ref.live(s))
def emit(q):
    return q[0], q[1]
def decode(q):
    o = []
    for b in range(4):
        e = np.zeros((128, 128, 4), np.float32); e[np.arange(128), np.arange(128), b] = 1
        o.append(mx_ref.matmul(mx_ref.quantize(e.reshape(128, 512).astype(BF)), q))
    return np.stack(o, axis=2).reshape(128, -1)
def f(rng, *shape):
    return mx_ref.flush((rng.standard_normal(shape, dtype=np.float32) * np.exp2(rng.integers(-2, 3, shape[:-1] + (1,)))).astype(BF))
def wide(rng, *shape, cols=0):
    v = rng.standard_normal(shape, dtype=np.float32) * np.exp2(rng.integers(-12, 13, shape)).astype(np.float32)
    if cols: v *= np.repeat(np.exp2(rng.integers(-cols, cols + 1, shape[:-2] + (1, shape[-1] // 4))) * (rng.random(shape[:-2] + (1, shape[-1] // 4)) > 0.0625), 4, axis=-1).astype(np.float32)
    return mx_ref.flush(v.astype(BF))
T, C = 384, 96
def best(s):
    return np.argsort(-(s + np.float32(0)), kind="stable")[:C]
def quant(u, v):
    qu = [mx_ref.quantize(np.ascontiguousarray(u[r])) for r in range(N)]
    return qu, [[mx_ref.quantize(np.ascontiguousarray(cut(v[r], i))) for i in range(4)] for r in range(N)]
def layer(q, qu, qv):
    e = best(mx_ref.matmul(qu, q)[0])
    old = pick(q, e)
    a = np.stack([mx_ref.matmul(t, old) for t in qv], axis=2)
    new = np.maximum(a, np.float32(0)) * np.float32(0.05) + decode(old).reshape(128, C, 4)
    return e, new.reshape(128, -1).astype(BF)
def setup_inputs(rng):
    u = np.zeros((N, 128, 512), BF)
    u[:, :, :4] = f(rng, N, 128, 4)
    return {"x": f(rng, N, 128, 4 * T), "u": u, "v": f(rng, N, 128, 2048), "w": f(rng, N, 128, 512)}
def setup_inputs_spread(rng):
    d = setup_inputs(rng)
    d["x"] = wide(rng, N, 128, 4 * T, cols=3)
    return d
def setup_inputs_ties(rng):
    d = setup_inputs(rng)
    d["x"] = np.stack([cols(d["x"][r], rng.permutation(T) % 5 - 1) for r in range(N)])
    d["u"][1::2] = 0
    return d
def setup_inputs_again(rng):
    d = setup_inputs(rng)
    x, u = d["x"].astype(np.float32).reshape(N, 128, T, 4), np.zeros((N, 128, 512), np.float32)
    good = np.stack([rng.permutation(T) < C for r in range(N)])
    x[:, :32] = (1 + rng.random((N, 32, T, 4))) * np.where(good, 1.0, -1.0)[:, None, :, None]
    u[:, :32, :4] = 1 + rng.random((N, 32, 4))
    d["x"], d["u"] = x.reshape(N, 128, 4 * T).astype(BF), u.astype(BF)
    return d
def setup_inputs_other(rng):
    d = setup_inputs(rng)
    x, u = d["x"].astype(np.float32).reshape(N, 128, T, 4), np.zeros((N, 128, 512), np.float32)
    v = d["v"].astype(np.float32).reshape(N, 128, 4, 128, 4)
    large = np.stack([rng.permutation(T) < C for r in range(N)])
    x[:, :16] = (1 + rng.random((N, 16, T, 4))) * np.where(large, 16.0, 1.0)[:, None, :, None]
    x[:, 16:32] = (0.25 + 0.25 * rng.random((N, 16, T, 4))) * rng.choice([-1.0, 1.0], (N, 16, T, 4))
    u[:, :16, :4] = 1 + rng.random((N, 16, 4))
    u[:, 16:32, :4] = -1 - rng.random((N, 16, 4))
    v[:, :, :, 16:32] = 0
    v[:, :16, :, 16:32] = 256 * (1 + rng.random((N, 16, 4, 16, 4)))
    d["x"], d["u"], d["v"] = x.reshape(N, 128, 4 * T).astype(BF), u.astype(BF), v.reshape(N, 128, 2048).astype(BF)
    return d
def setup_inputs_neg(rng):
    d = setup_inputs(rng)
    d["x"] = np.abs(d["x"].astype(np.float32)).astype(BF)
    d["v"] = (-np.abs(d["v"].astype(np.float32))).astype(BF)
    return d
def check_inputs(d):
    b = []
    for k in ("x", "u", "v", "w"):
        a = np.abs(d[k].astype(np.float32))
        if not (np.isfinite(a).all() and ((a == 0) | (a >= 2.0 ** -30) & (a <= 2.0 ** 30)).all()): b.append("a value of " + k)
    if (d["u"][:, :, 4:].astype(np.float32) != 0).any(): b.append("u has numbers behind its column 0")
    if b: return b
    qu, qv = quant(d["u"], d["v"])
    for r in range(N):
        q = mx_ref.quantize(np.ascontiguousarray(d["x"][r]))
        for k in (1, 2):
            e, new = layer(q, qu[(r + k) % N], qv[(r + k) % N])
            a = np.abs(new.astype(np.float32)).reshape(16, 8, C, 4).max(axis=(1, 3))
            if not ((a == 0) | (a >= 2.0 ** -30) & (a <= 2.0 ** 30)).all(): return ["a number of a made column"]
            q = put(q, e, mx_ref.quantize(new))
    return b
def reference(x, u, v, w):
    oc, osc = np.zeros((N, 128, 4 * T), np.uint8), np.zeros((N, 16, T), np.uint8)
    li, y = np.zeros((N, 2, C), np.float32), np.zeros((N, 128, T), np.float32)
    qu, qv = quant(u, v)
    for d in range(N):
        r = (d - 2) % N
        q = mx_ref.quantize(np.ascontiguousarray(x[r]))
        for k in (1, 2):
            s = (r + k) % N
            e, new = layer(q, qu[s], qv[s])
            q = put(q, e, mx_ref.quantize(new))
            li[d, k - 1] = e
        oc[d], osc[d] = emit(q)
        y[d] = mx_ref.matmul(mx_ref.quantize(np.ascontiguousarray(w[d])), q)
    return {"oc": oc, "osc": osc, "li": li, "y": y}

@@ -1,0 +1,471 @@
+import numpy as np
+from concourse.bass import DstId, RemoteDMATransfer
+from concourse.mybir import dt, AluOpType, AxisListType, ActivationFunctionType
+
+F8 = "float8_e4m3fn_x4"
+CH = 96
+NT = 384
+HALF = CH + NT
+T0 = HALF + CH
+NZ = 226
+
+
+def sb(n, d):
+    return ("sbuf", [128, n], d)
+
+
+def codes(**names):
+    d = {}
+    for k, n in names.items():
+        d[k], d[k + "s"] = sb(n, F8), sb(n, "uint8")
+    return d
+
+
+SCRATCH = {
+    "ps": ("psum", [128, 4096], "float32"),
+    "ub": sb(512, "bfloat16"), "xb": sb(4 * NT, "bfloat16"), "vb": sb(2048, "bfloat16"), "wb": sb(512, "bfloat16"),
+    "ones": sb(128, "bfloat16"), "z16": sb(8, "uint16"), "eb": sb(520, "bfloat16"), "urb": sb(512, "bfloat16"),
+    "tri": sb(128, "bfloat16"), "q0": sb(128, "bfloat16"), "qm": sb(128, "bfloat16"), "pp": sb(128, "bfloat16"),
+    "pm": sb(128, "bfloat16"), "wa": sb(128, "bfloat16"), "kc": sb(48, "float32"), "jj": sb(24, "float32"),
+    "jx": sb(24, "float32"), "ab": sb(48, "float32"), "jbp": sb(1, "float32"), "ip": sb(1, "float32"),
+    "ip1": sb(1, "float32"), "ip2": sb(1, "float32"), "ip3": sb(1, "float32"), "p16f": sb(1, "float32"),
+    "c75": sb(1, "bfloat16"), "j96": sb(4, "float32"), "c88": sb(96, "float32"), "tha": sb(96, "float32"),
+    "thr": sb(96, "float32"), "w2b": sb(512, "bfloat16"), "zb": sb(4 * NZ, "bfloat16"),
+    "sc": sb(3, "float32"), "dl": sb(3, "float32"), "mt": sb(NT, "float32"), "cmp": sb(4 * NT, "bfloat16"),
+    "sg": sb(NT, "bfloat16"), "kl": sb(48, "float32"), "x0": sb(48, "float32"), "wx": sb(560, "bfloat16"),
+    "xo": sb(512, "bfloat16"), "ak": sb(4, "float32"), "offn": sb(3, "uint16"), "offs": ("dram", [128, 3], "uint16"),
+    "lst1": sb(6, "uint16"), "off2f": sb(24, "float32"), "off2": sb(24, "uint16"),
+    "lin": sb(6, "uint16"), "offd": ("dram", [128, 3], "uint16"), "off1a": sb(24, "uint16"), "off1": sb(24, "uint16"),
+    "off1f": sb(24, "float32"),
+    "hrb": sb(4 * CH, "float32"), "hr0": sb(4 * NT, "float32"), "hr1": sb(4 * CH, "float32"),
+    "hb": sb(512, "bfloat16"), "hx": sb(4 * HALF, "bfloat16"),
+    "yb": sb(NT, "float32"), "lif": sb(6, "float32"), "lir": sb(96, "float32"),
+}
+SCRATCH.update(codes(uq=128, ur1=128, ur2=128, t0=NT, vq=512, wq=128, qe=CH + 512, w2=128, zq=NZ, cq=NT, wxq=140,
+                     xoq=128, q1=CH, m1=128, big=2 * HALF, t1=NT, oq=NT, uin=144))
+SEMAPHORES = ["sV", "sT", "sS", "sG", "du", "dx0", "dx1", "dx2", "dof", "dv0", "dv1", "dv2", "dv3", "dw", "doff", "dst",
+              "au", "aq", "at", "am", "al", "ao", "go", "go2", "ls"]
+
+OP = AluOpType
+AF = ActivationFunctionType
+BIG1, BIG16, BIG32 = 1.5 * 2.0 ** 23, 1.5 * 2.0 ** 27, 1.5 * 2.0 ** 28
+ULP = 1.03125 * 2.0 ** -24
+TINY = 1e-37
+C05 = 13421773 * 2.0 ** -28
+BANKS = ["b%d" % k for k in range(8)]
+
+
+def sched(g, T):
+    eng = {"V": g.vector, "T": g.tensor, "S": g.scalar, "G": g, "Y": g.sync}
+    cnt = {"V": 0, "T": 0, "S": 0, "G": 0}
+    wr, rd, seen = {}, {}, {}
+
+    def wait(q, reads, writes):
+        req = {}
+        for k in reads:
+            for qq, s, v in wr.get(k, []):
+                req[s] = max(req.get(s, 0), v)
+            if k in BANKS:
+                for qq, s, v in rd.get(k, []):
+                    if qq != q:
+                        req[s] = max(req.get(s, 0), v)
+        for k in writes:
+            for qq, s, v in wr.get(k, []) + rd.get(k, []):
+                if qq != q or q != "T":
+                    req[s] = max(req.get(s, 0), v)
+        for s, v in req.items():
+            if seen.get((q, s), 0) < v:
+                eng[q].wait_ge(T.sem[s], v)
+                seen[(q, s)] = v
+
+    def note(q, s, v, reads, writes):
+        for k in reads:
+            rd.setdefault(k, []).append((q, s, v))
+        for k in writes:
+            wr[k] = [(q, s, v)]
+            rd[k] = []
+
+    def op(q, call, reads, writes):
+        wait(q, reads, writes)
+        cnt[q] += 1
+        call(eng[q]).then_inc(T.sem["s" + q], 1)
+        note(q, "s" + q, cnt[q], reads, writes)
+
+    def dma(q, pairs, s, v, reads, writes):
+        wait(q, reads, writes)
+        for o, i in pairs:
+            eng[q].dma_start(o, i).then_inc(T.sem[s], 16)
+        note("dma", s, v, reads, writes)
+
+    def arrive(s, v, keys):
+        for k in keys:
+            wr[k] = [("far", s, v)]
+    return op, dma, arrive, wait, cnt
+
+
+def rank_program(g, core, T, topo):
+    r = T.rank_of(core)
+    if r is None:
+        return
+    n = len(T.cores)
+    nxt, nx2, prv = T.cores[(r + 1) % n], T.cores[(r + 2) % n], T.cores[(r - 1) % n]
+    op, dma, arrive, wait, cnt = sched(g, T)
+    ps = T.ps
+    loc = [0]
+
+    def half(dst, k):
+        e = topo.engines(core, dst)
+        return e[:len(e) // 2] if k == 0 else e[len(e) // 2:]
+
+    def bits(es):
+        return sum(1 << e for e in es)
+
+    def send(dst, out, src, sem, es, reads):
+        wait("G", reads, [])
+        rid, pid, _ = topo.addr(dst)
+        g.remote_dma(out, src, T.sem[sem], T.sem["ls"], pid, rid, bits(es))
+        loc[0] += len(es)
+
+    def u8(name, a, b):
+        return T[name][:, a:b].bitcast(dt.uint8)
+
+    arrive("au", 8, ["uin"])
+    arrive("aq", 32, ["qin"])
+    arrive("at", 32, ["bt"])
+    arrive("am", 32, ["bm"])
+    arrive("al", 8, ["lin"])
+    arrive("ao", 8, ["offd"])
+    arrive("go", 1, ["go"])
+    arrive("go2", 1, ["go2"])
+
+    def V(f, reads, writes):
+        op("V", f, reads, writes)
+
+    def S(f, reads, writes):
+        op("S", f, reads, writes)
+
+    def G(f, reads, writes):
+        op("G", f, reads, writes)
+
+    def memset(ap, c, key, after=()):
+        V(lambda e: e.memset(ap, c), list(after), [key])
+
+    def iota(ap, pattern, key, cm=0, base=0):
+        G(lambda e: e.iota(ap, pattern, base, cm, allow_small_or_imprecise_dtypes=True), [], [key])
+
+    def ts(out, in0, s1, o, reads, key):
+        V(lambda e: e.tensor_scalar(out, in0, s1, None, o), reads, [key])
+
+    def tt(out, in0, in1, o, reads, key):
+        V(lambda e: e.tensor_tensor(out, in0, in1, o), reads, [key])
+
+    def cp(out, in_, reads, key):
+        V(lambda e: e.tensor_copy(out, in_), reads, [key])
+
+    def act(out, in_, f, bias, scale, reads, key):
+        S(lambda e: e.activation(out, in_, f, bias=bias, scale=scale), reads, [key])
+
+    def zero(out, w, key):
+        S(lambda e: e.activation(out, T.ub[:, 8:8 + w], AF.Copy), ["ubz"], [key])
+
+    def quant(out, a, b, src, reads, key):
+        V(lambda e: e.quantize_mx(T[out][:, a:b], T[out + "s"][:, a:b], src), reads, [key])
+
+    def mm(bank, w, L, l0, R, r0, start, stop, reads):
+        op("T", lambda e: e.matmul_mx(ps[:, 512 * bank:512 * bank + w], T[L][:, l0:l0 + 128], T[L + "s"][:, l0:l0 + 128],
+                                      T[R][:, r0:r0 + w], T[R + "s"][:, r0:r0 + w], start, stop), reads, ["b%d" % bank])
+
+    def B(bank, a, b):
+        return ps[:, 512 * bank + a:512 * bank + b]
+
+    def pick_c(dst, d0, w, src, a, b, off, o0, reads, key):
+        V(lambda e: e.tensor_copy(T[dst][:, d0:d0 + w].bitcast(dt.uint32),
+                                  T[src][:, a:b].bitcast(dt.uint32).indirect(T[off][:, o0:o0 + w // 16])), reads, [key])
+
+    def pick_s(dst, d0, w, src, a, b, off, o0, reads, key):
+        S(lambda e: e.activation(T[dst + "s"][:, d0:d0 + w], T[src + "s"][:, a:b].indirect(T[off][:, o0:o0 + w // 16]),
+                                 AF.Copy), reads, [key])
+
+    def hk(key, k=4):
+        return [key + str(i) for i in range(k)]
+
+    dma("Y", [(T.ub[:, 0:8], T.u[:, 0:8])], "du", 16, [], ["ub"])
+    for c in range(3):
+        dma("Y", [(T.xb[:, 512 * c:512 * c + 512], T.x[:, 512 * c:512 * c + 512])], "dx%d" % c, 16, [], ["xb%d" % c])
+
+    memset(T.ub[:, 8:512], 0.0, "ubz")
+    memset(T.ones[:], 1.0, "ones")
+    iota(T.jj[:], [[0, 6], [128, 4]], "jj", 1)
+    iota(T.ip[:], [[0, 1]], "ip", 2)
+    G(lambda e: e.affine_select(T.c75[:], T.ub[:, 8:9], [[1, 1]], OP.not_equal, -7.5, 0, 1), ["ubz"], ["c75"])
+    iota(T.q0[:], [[0, 8], [1, 16]], "q0")
+    quant("uq", 0, 128, T.ub[:], ["ub", "ubz"], "uq")
+    memset(T.zb[:], 0.0, "zbz")
+    memset(T.z16[:], 0, "z16")
+    quant("uin", 0, 128, T.zb[:, 0:512], ["zbz"], "uinz")
+    wait("G", ["uq"], [])
+    rid, pid, _ = topo.addr(prv)
+    e0 = half(prv, 0)
+    g.remote_dma_fused([RemoteDMATransfer(dst_ids=[DstId(rid=rid, pnc=pid)], dma_engine_mask=bits(e0[:4]), remote_sem=T.sem["au"],
+                                          src=u8("uq", 0, 2), dst=u8("uin", 128, 130)),
+                        RemoteDMATransfer(dst_ids=[DstId(rid=rid, pnc=pid)], dma_engine_mask=bits(e0[4:]), remote_sem=T.sem["au"],
+                                          src=T.uqs[:, 0:8], dst=T.uins[:, 128:136])], local_sem=T.sem["ls"])
+    loc[0] += len(e0)
+    zero(T.eb[:, 0:504], 504, "ebz")
+    zero(T.eb[:, 504:520], 16, "ebz2")
+    G(lambda e: e.affine_select(T.eb[:, 4:516:4], T.ones[:], [[-1, 128]], OP.is_equal, 0.0, 0, 1), ["ones", "ebz", "ebz2"], ["ebi"])
+    G(lambda e: e.affine_select(T.tri[:], T.ones[:], [[1, 128]], OP.is_gt, 0.0, 0, -1), ["ones"], ["tri"])
+    iota(T.kc[:], [[0, 2], [16, 6], [0, 4]], "kc")
+    iota(T.pp[:], [[1, 128]], "pp")
+    iota(T.j96[:], [[128, 4]], "j96", 1, CH)
+    act(T.jx[:], T.jj[:], AF.Identity, BIG32, 1.0, ["jj"], "jx")
+    act(T.ip1[:], T.ip[:], AF.Identity, -15.0, 1.0, ["ip"], "ip1")
+    act(T.ab[:, 0:24], T.jx[:], AF.Identity, -BIG32, 1.0, ["jx"], "aba")
+    act(T.ip2[:], T.ip1[:], AF.Identity, BIG1, 1.0 / 32, ["ip1"], "ip2")
+    act(T.jbp[:], T.ab[:, 0:1], AF.Identity, T.jj[:, 0:1], -1.0, ["aba", "jj"], "jbp")
+    act(T.ip3[:], T.ip2[:], AF.Identity, -BIG1, 1.0, ["ip2"], "ip3")
+    act(T.ab[:, 24:48], T.ub[:, 8:32], AF.Identity, T.jbp[:, 0:1], 1.0, ["ubz", "jbp"], "abb")
+    act(T.cmp[:, 3:4 * NT:4], T.ub[:, 8:8 + NT], AF.Identity, T.c75[:, 0:1], 1.0, ["ubz", "c75"], "cmk")
+    act(T.p16f[:], T.ip3[:], AF.Identity, T.jj[:, 0:1], -16.0, ["ip3", "jj"], "p16f")
+    zero(T.wx[:, 51:560:4], 128, "wxz")
+    act(T.qm[:], T.q0[:], AF.Identity, -7.5, 1.0, ["q0"], "qm")
+    for t in range(4):
+        for a in range(2):
+            k = 24 if t < 3 else 12
+            act(T.zb[:, 388 * a + 8 + t:388 * a + 8 + 16 * k:16], T.ones[:, 0:k], AF.Copy, 0.0, 1.0, ["ones", "zbz", "uinz"], "zo%d%d" % (a, t))
+    act(T.zb[:, 888:891], T.ub[:, 8:11], AF.Identity, T.jbp[:, 0:1], 1.0, ["ubz", "jbp", "zbz"], "zba")
+    act(T.zb[:, 896:899], T.ab[:, 0:3], AF.Copy, 0.0, 1.0, ["aba", "zbz"], "zbb")
+
+    def EQ(b):
+        quant("qe", CH + 128 * b, CH + 128 * b + 128, T.eb[:, 4 - b:516 - b], ["ebz", "ebz2", "ebi"], "eq%d" % b)
+    for c in range(3):
+        quant("t0", 128 * c, 128 * c + 128, T.xb[:, 512 * c:512 * c + 512], ["xb%d" % c], "t0%d" % c)
+        if c < 2:
+            EQ(c)
+    t0 = hk("t0", 3)
+    send(nx2, u8("big", T0, T0 + NT), u8("t0", 0, NT), "at", topo.engines(core, nx2), t0)
+    send(nx2, T.bigs[:, T0:T0 + NT], T.t0s[:, 0:NT], "at", topo.engines(core, nx2), [])
+    g.sem_inc(T.sem["go"], 1)
+    for i in range(4):
+        dma("Y", [(T.vb[:, 512 * i:512 * i + 512], T.v[:, 512 * i:512 * i + 512])], "dv%d" % i, 16, ["go", "uin"], ["vb%d" % i])
+
+    ROW = (0, 6, 7)
+    SC = 126
+
+    def col(c, tok, ur, keys, at=0):
+        mm(1 + c, 128, tok, 128 * c, ur, at, True, True, keys)
+
+    def row(c, tok, ur, keys):
+        mm(ROW[c], 128, ur, 0, tok, 128 * c, True, True, keys)
+
+    def slot(c, t):
+        return T.cmp[:, 512 * c + t:512 * c + 512:4]
+
+    def against(c, t):
+        if c == t:
+            tt(slot(c, c), B(ROW[c], 0, 128), T.mt[:, 128 * c:128 * c + 128], OP.is_lt, ["b%d" % ROW[c], "mt%d" % c], "cm%d%d" % (c, c))
+        else:
+            ts(slot(c, t), B(ROW[c], 0, 128), T.sc[:, t:t + 1], OP.is_le if t < c else OP.is_lt, ["b%d" % ROW[c], "sc%d" % t], "cm%d%d" % (c, t))
+
+    def sign(c, t):
+        k = c + t - 1
+        act(T.sg[:, 128 * k:128 * k + 128], B(ROW[c], 0, 128), AF.Sign, T.sc[:, t:t + 1], -1.0, ["b%d" % ROW[c], "sc%d" % t], "sg%d" % k)
+
+    def relu(c, t):
+        k = c + t - 1
+        act(slot(c, t), T.sg[:, 128 * k:128 * k + 128], AF.Relu, 0.0, 1.0, ["sg%d" % k], "cm%d%d" % (c, t))
+
+    def score(a, b):
+        S(lambda e: e.activation(T.sc[:, a:b], ps[:, 512 * a + 512 + SC:512 * b + 512:512], AF.Copy),
+          ["b%d" % (1 + c) for c in range(a, b)], ["sc%d" % c for c in range(a, b)])
+
+    def step(a, b):
+        S(lambda e: e.activation(T.dl[:, a:b], ps[:, 512 * a + 512 + SC:512 * b + 512:512], AF.Abs, bias=TINY, scale=ULP),
+          ["b%d" % (1 + c) for c in range(a, b)], ["dl%d" % c for c in range(a, b)])
+
+    def shift(c):
+        act(T.mt[:, 128 * c:128 * c + 128], T.tri[:], AF.Identity, T.sc[:, c:c + 1], T.dl[:, c:c + 1], ["tri", "sc%d" % c, "dl%d" % c], "mt%d" % c)
+
+    def pack(c):
+        quant("cq", 128 * c, 128 * c + 128, T.cmp[:, 512 * c:512 * c + 512], hk("cm%d" % c, 3) + ["cmk"], "cq%d" % c)
+
+    def position(c):
+        mm(4, 128, "cq", 128 * c, "zq", (2, 98, 0)[c], c == 2, c == 0, ["cq%d" % c, "zq"])
+
+    def R(i, bank, q, q0, w, out, w2, keys):
+        mm(bank, w, "vq", 128 * i, q, q0, True, True, keys + ["vq%d" % i])
+        act(T[out][:, w2 * i:w2 * i + w2], B(bank, 0, w2), AF.Relu, 0.0, C05, ["b%d" % bank], out + str(i))
+
+    def D(i, bank, q, q0, w, keys):
+        mm(bank, w, "qe", CH + 128 * i, q, q0, True, True, keys + ["eq%d" % i])
+
+    def add(i, bank, h, c0, w, hr, key):
+        tt(T[h][:, 4 * c0 + i:4 * (c0 + w):4], T[hr][:, w * i:w * i + w], B(bank, 0, w), OP.add, [hr + str(i), "b%d" % bank], key + str(i))
+
+    def D0(b):
+        D(b, b, "big", T0, NT, ["bt"])
+
+    def R0(i, bank):
+        R(i, bank, "big", T0, NT, "hr0", NT, ["bt"])
+
+    def A0(i):
+        add(i, i, "hx", CH, NT, "hr0", "h0")
+
+    def VQ(i):
+        quant("vq", 128 * i, 128 * i + 128, T.vb[:, 512 * i:512 * i + 512], ["vb%d" % i], "vq%d" % i)
+
+    uk = ["uin", "uinz"]
+    EQ(2)
+    for c in range(3):
+        col(c, "t0", "uin", ["t0%d" % c] + uk, 2)
+    pick_s("ur1", 0, 128, "uin", 128, 130, "z16", 0, uk + ["z16"], "ur1s")
+    pick_c("ur1", 0, 128, "uin", 128, 130, "z16", 0, uk + ["z16"], "ur1")
+    for c in (2, 0, 1):
+        row(c, "t0", "ur1", ["t0%d" % c, "ur1", "ur1s"])
+    quant("zq", 0, NZ, T.zb[:], ["zbz", "zba", "zbb"] + hk("zo0") + hk("zo1"), "zq")
+    score(0, 3), step(0, 3), shift(2), sign(0, 2), sign(1, 2), shift(1), shift(0), relu(1, 2), relu(0, 2)
+    for c, t in ((2, 0), (2, 1), (2, 2), (0, 1), (1, 0), (1, 1)):
+        against(c, t)
+    pack(2), against(0, 0), pack(1), pack(0)
+    position(2), position(1), position(0)
+    D0(0)
+    for t in range(4):
+        act(T.urb[:, t:512:4], T.ub[:, 8:136], AF.Identity, T.ub[:, t:t + 1], 1.0, ["ub", "ubz"], "urb%d" % t)
+    act(T.wa[:], T.q0[:], AF.Abs, T.p16f[:, 0:1], -1.0, ["q0", "p16f"], "wa")
+    act(T.c88[:, 0:48], T.ones[:, 0:48], AF.Identity, CH - 9.0, 1.0, ["ones"], "c88a")
+    act(T.c88[:, 48:96], T.ones[:, 0:48], AF.Identity, CH - 1.5, 1.0, ["ones"], "c88b")
+    zero(T.hb[:, 4 * CH:512], 128, "hbz")
+    zero(T.xo[:, 96:512], 416, "xoz")
+    V(lambda e: e.tensor_scalar(T.kl[:], B(4, 0, 48), BIG16, BIG16, OP.add, OP.subtract), ["b4"], ["kl"])
+    V(lambda e: e.tensor_scalar(T.ak[:], B(4, 48, 52), CH - 0.5, 1000.0, OP.subtract, OP.mult), ["b4"], ["ak"])
+
+    def offn(t):
+        V(lambda e: e.tensor_scalar(T.offn[:, t:t + 1], B(4, 48 + t, 49 + t), T.ak[:, t:t + 1], T.j96[:, t:t + 1], OP.max, OP.min),
+          ["b4", "ak", "j96"], ["offn%d" % t])
+    tt(T.x0[:], T.kl[:], T.kc[:], OP.is_equal, ["kl", "kc"], "x0")
+    for t in range(3):
+        V(lambda e, t=t: e.tensor_scalar(T.wx[:, 48 + t:560:4], T.qm[:], T.kl[:, t:t + 1], B(4, t, t + 1), OP.add, OP.is_equal),
+          ["kl", "qm", "b4"], ["wx%d" % t])
+        if t == 1:
+            tt(T.wx[:, 0:48], T.x0[:], T.ab[:], OP.mult, ["x0", "aba", "abb"], "wxx")
+    offn(0)
+    quant("wxq", 0, 140, T.wx[:], ["wxz", "wx0", "wx1", "wx2", "wxx"], "wxq")
+    mm(5, 128, "wxq", 12, "wxq", 0, True, False, ["wxq"])
+    mm(5, 128, "wxq", 12, "wxq", 6, False, True, ["wxq"])
+    D0(1)
+    offn(1), offn(2), EQ(3)
+    dma("Y", [(T.offs[k:128:8, :], T.offn[16 * k:16 * k + 16, :]) for k in range(8)], "dof", 128, hk("offn", 3), ["offs"])
+    dma("Y", [(T.wb[:], T.w[:])], "dw", 16, ["go2"], ["wb"])
+    cp(T.lst1[:], B(5, 0, 6), ["b5"], "lst1")
+    pick_s("q1", 0, CH, "t0", 0, NT, "lst1", 0, t0 + ["lst1"], "q1s")
+    pick_c("q1", 0, CH, "t0", 0, NT, "lst1", 0, t0 + ["lst1"], "q1")
+    send(nxt, u8("qe", 0, CH), u8("q1", 0, CH), "aq", topo.engines(core, nxt), ["q1"])
+    send(nxt, T.qes[:, 0:CH], T.q1s[:, 0:CH], "aq", topo.engines(core, nxt), ["q1s"])
+    g.sem_inc(T.sem["go2"], 1)
+    send(nx2, T.lin[:], T.lst1[:], "al", half(nx2, 0), ["lst1"])
+    send(nx2, T.offd[:], T.offs[:], "ao", half(nx2, 0), ["offs"])
+    VQ(0), VQ(1), VQ(2), VQ(3)
+    for t in range(4):
+        act(T.w2b[:, t:512:4], T.wa[:], AF.Relu, float(HALF), -float(HALF), ["wa"], "w2b%d" % t)
+    R0(0, 7), R0(1, 6), R0(2, 2)
+    quant("ur2", 0, 128, T.urb[:], hk("urb"), "ur2")
+    quant("w2", 0, 128, T.w2b[:], hk("w2b"), "w2")
+    A0(0)
+    G(lambda e: e.affine_select(T.tha[:], T.c88[:], [[-16, 24], [128, 4]], OP.is_ge, CH + 392.5, 0, 1), ["c88a", "c88b"], ["tha"])
+    G(lambda e: e.affine_select(T.thr[:], T.tha[:], [[16, 24], [-128, 4]], OP.is_ge, CH + 392.5, 15, -1), ["tha"], ["thr"])
+
+    def RB(i, bank):
+        R(i, bank, "qe", 0, 128, "hrb", CH, ["qin", "eq0"])
+
+    def DB(i, bank):
+        D(i, bank, "qe", 0, 128, ["qin", "eq0"])
+
+    def AB(i, bank):
+        add(i, bank, "hb", 0, CH, "hrb", "hb")
+    A0(1)
+    RB(0, 4), RB(1, 5), RB(2, 3), RB(3, 6), DB(0, 7), DB(1, 4), DB(2, 5), DB(3, 3)
+    AB(0, 7), AB(1, 4), AB(2, 5), AB(3, 3)
+    quant("m1", 0, 128, T.hb[:], ["hbz"] + hk("hb"), "m1")
+    send(nxt, u8("big", HALF, HALF + CH), u8("m1", 0, CH), "am", topo.engines(core, nxt), ["m1"])
+    send(nxt, T.bigs[:, HALF:HALF + CH], T.m1s[:, 0:CH], "am", topo.engines(core, nxt), [])
+    dma("Y", [(T.off1a[16 * h:16 * h + 16, :], T.offd[:]) for h in range(8)], "doff", 128, ["offd"], ["off1a"])
+    R0(3, 6), D0(2), D0(3)
+    act(T.pm[:], T.pp[:], AF.Identity, -7.5, 1.0, ["pp"], "pm")
+    quant("wq", 0, 128, T.wb[:], ["wb"], "wq")
+    A0(2)
+    A0(3)
+    quant("big", CH + 192, HALF, T.hx[:, 4 * CH + 768:4 * HALF], hk("h0"), "bh0b")
+    for t in range(3):
+        cp(T.off1[:, 8 * t:8 * t + 8], T.off1a[:, t:24:3], ["off1a"], "off1%d" % t)
+    stores = [0]
+
+    def store(q, pairs, reads):
+        dma(q, pairs, "dst", 0, reads, [])
+        stores[0] += 16 * len(pairs)
+
+    mk = ["bt", "bm"]
+    for c in range(3):
+        pick_s("t1", 128 * c, 128, "big", HALF, 2 * HALF, "off1", 8 * c, mk + ["off1%d" % c], "t1s%d" % c)
+        pick_c("t1", 128 * c, 128, "big", HALF, 2 * HALF, "off1", 8 * c, mk + ["off1%d" % c], "t1c%d" % c)
+        for f in (col, row):
+            f(c, "t1", "ur2", ["t1c%d" % c, "t1s%d" % c, "ur2"])
+
+    def N(what, i, bank):
+        if what == "D":
+            D(i, bank, "big", HALF, 128, mk)
+        else:
+            R(i, bank, "big", HALF, 128, "hr1", CH, mk)
+
+    score(0, 2), step(0, 2), score(2, 3), step(2, 3), shift(0)
+    cp(T.off1f[:], T.off1[:], hk("off1", 3), "off1f")
+    against(0, 1), against(1, 0)
+    sign(1, 2), shift(2)
+    against(2, 0), against(2, 1), against(0, 0)
+    sign(0, 2), shift(1), relu(1, 2), relu(0, 2)
+    quant("big", CH, CH + 192, T.hx[:, 4 * CH:4 * CH + 768], hk("h0"), "bh0a")
+    against(2, 2), against(1, 1), pack(2)
+    cp(T.lif[:], T.lin[:], ["lin"], "lif")
+    pack(1), pack(0)
+    store("Y", [(T.li[0:1, 16 * k:16 * k + 16], T.lif[0:16, k:k + 1]) for k in range(6)], ["lif"])
+    N("R", 0, 1), N("D", 0, 2), N("R", 1, 5), N("D", 1, 3)
+    N("R", 2, 7), position(2), N("R", 3, 6), position(1), position(0), N("D", 2, 1), N("D", 3, 5)
+    add(0, 2, "hx", 0, CH, "hr1", "h1")
+    add(1, 3, "hx", 0, CH, "hr1", "h1")
+    tt(T.xo[:, 0:96], T.thr[:], B(4, 0, 96), OP.is_le, ["thr", "b4"], "xo")
+
+    def rowlist(t):
+        ts(T.wx[:, 48 + t:560:4], T.pm[:], B(4, t, t + 1), OP.is_equal, ["pm", "b4", "wxq"], "wx%d" % t)
+    rowlist(0)
+    quant("xoq", 0, 128, T.xo[:], ["xoz", "xo"], "xoq")
+    mm(7, 128, "w2", 0, "xoq", 0, True, True, ["xoq", "w2"])
+    add(2, 1, "hx", 0, CH, "hr1", "h1")
+    add(3, 5, "hx", 0, CH, "hr1", "h1")
+    rowlist(1)
+    quant("big", 0, 128, T.hx[:, 0:512], hk("h0") + hk("h1") + ["bh0a"], "bh1")
+    tt(T.off2f[:], T.off1f[:], B(7, 0, 24), OP.add, ["off1f", "b7"], "off2f")
+    rowlist(2)
+    cp(T.off2[:], T.off2f[:], ["off2f"], "off2")
+    quant("wxq", 12, 140, T.wx[:, 48:560], ["wxz", "wx0", "wx1", "wx2"], "wxq")
+    mm(0, 128, "zq", 98, "wxq", 12, True, False, ["wxq", "zq"])
+    mm(0, 128, "zq", 96, "wxq", 12, False, True, ["wxq", "zq"])
+    al = ["bh0a", "bh0b", "bh1", "off2"] + mk
+    for c in range(3):
+        pick_s("oq", 128 * c, 128, "big", 0, 2 * HALF, "off2", 8 * c, al, "oqs%d" % c)
+        pick_c("oq", 128 * c, 128, "big", 0, 2 * HALF, "off2", 8 * c, al, "oq%d" % c)
+        mm((5, 6, 7)[c], 128, "wq", 0, "oq", 128 * c, True, True, ["wq", "oq%d" % c, "oqs%d" % c])
+        if c != 1:
+            a = max(128 * c - 128, 0)
+            store("Y", [(T.oc[:, 4 * a:512 * c + 512], u8("oq", a, 128 * c + 128))], ["oq1", "oq2"] if c else ["oq0"])
+    for c in range(2):
+        act(T.yb[:, 128 * c:128 * c + 128], B(5 + c, 0, 128), AF.Copy, 0.0, 1.0, ["b%d" % (5 + c)], "yb%d" % c)
+    cp(T.lir[:], B(0, 0, 96), ["b0"], "lir")
+    cp(T.yb[:, 256:384], B(7, 0, 128), ["b7"], "yb2")
+    store("Y", [(T.osc[4 * k:4 * k + 4, :], T.oqs[32 * k:32 * k + 4, :]) for k in range(4)], hk("oqs", 3))
+    for a, b in ((0, 2), (2, 3)):
+        store("Y", [(T.y[:, 128 * a:128 * b], T.yb[:, 128 * a:128 * b])], ["yb%d" % c for c in range(a, b)])
+    store("S", [(T.li[1:2, :], T.lir[126:127, :])], ["lir"])
+
+    for q in ("V", "T", "S", "G"):
+        g.wait_ge(T.sem["s" + q], cnt[q])
+    g.wait_ge(T.sem["ls"], loc[0])
+    g.wait_ge(T.sem["dst"], stores[0])

@@ -5,9 +5,11 @@ from concourse.mybir import dt, AluOpType, AxisListType, ActivationFunctionType
 F8 = "float8_e4m3fn_x4"
 CH = 96
 NT = 384
-HALF = CH + NT
-T0 = HALF + CH
-NZ = 226
+HO = 512
+TRI, ONE = 512, 640
+ZO, ZU, ZD, ZA, ZB, ZT, ZP, NZ = 70, 138, 206, 336, 352, 384, 392, 520
+NA = 16
+WX = 140 + NA
 
 
 def sb(n, d):
@@ -21,49 +23,55 @@ def codes(**names):
     return d
 
 
-SCRATCH = {
-    "ps": ("psum", [128, 4096], "float32"),
-    "ub": sb(512, "bfloat16"), "xb": sb(4 * NT, "bfloat16"), "vb": sb(2048, "bfloat16"), "wb": sb(512, "bfloat16"),
-    "ones": sb(128, "bfloat16"), "z16": sb(8, "uint16"), "eb": sb(520, "bfloat16"), "urb": sb(512, "bfloat16"),
-    "tri": sb(128, "bfloat16"), "q0": sb(128, "bfloat16"), "qm": sb(128, "bfloat16"), "pp": sb(128, "bfloat16"),
-    "pm": sb(128, "bfloat16"), "wa": sb(128, "bfloat16"), "kc": sb(48, "float32"), "jj": sb(24, "float32"),
-    "jx": sb(24, "float32"), "ab": sb(48, "float32"), "jbp": sb(1, "float32"), "ip": sb(1, "float32"),
-    "ip1": sb(1, "float32"), "ip2": sb(1, "float32"), "ip3": sb(1, "float32"), "p16f": sb(1, "float32"),
-    "c75": sb(1, "bfloat16"), "j96": sb(4, "float32"), "c88": sb(96, "float32"), "tha": sb(96, "float32"),
-    "thr": sb(96, "float32"), "w2b": sb(512, "bfloat16"), "zb": sb(4 * NZ, "bfloat16"),
-    "sc": sb(3, "float32"), "dl": sb(3, "float32"), "mt": sb(NT, "float32"), "cmp": sb(4 * NT, "bfloat16"),
-    "sg": sb(NT, "bfloat16"), "kl": sb(48, "float32"), "x0": sb(48, "float32"), "wx": sb(560, "bfloat16"),
-    "xo": sb(512, "bfloat16"), "ak": sb(4, "float32"), "offn": sb(3, "uint16"), "offs": ("dram", [128, 3], "uint16"),
-    "lst1": sb(6, "uint16"), "off2f": sb(24, "float32"), "off2": sb(24, "uint16"),
-    "lin": sb(6, "uint16"), "offd": ("dram", [128, 3], "uint16"), "off1a": sb(24, "uint16"), "off1": sb(24, "uint16"),
-    "off1f": sb(24, "float32"),
-    "hrb": sb(4 * CH, "float32"), "hr0": sb(4 * NT, "float32"), "hr1": sb(4 * CH, "float32"),
-    "hb": sb(512, "bfloat16"), "hx": sb(4 * HALF, "bfloat16"),
-    "yb": sb(NT, "float32"), "lif": sb(6, "float32"), "lir": sb(96, "float32"),
-}
-SCRATCH.update(codes(uq=128, ur1=128, ur2=128, t0=NT, vq=512, wq=128, qe=CH + 512, w2=128, zq=NZ, cq=NT, wxq=140,
-                     xoq=128, q1=CH, m1=128, big=2 * HALF, t1=NT, oq=NT, uin=144))
-SEMAPHORES = ["sV", "sT", "sS", "sG", "du", "dx0", "dx1", "dx2", "dof", "dv0", "dv1", "dv2", "dv3", "dw", "doff", "dst",
-              "au", "aq", "at", "am", "al", "ao", "go", "go2", "ls"]
+F, H, U = "float32", "bfloat16", "uint16"
+SCRATCH = {"ps": ("psum", [128, 4096], F)}
+SCRATCH.update({k: sb(n, d) for d, names in (
+    (H, dict(ub=896, xb=4 * NT, vb=2048, wb=512, eb=520, urb=512, q0=128, pp=128, wa=128, c75=1, zb=4 * NZ, k12=24, xw=1024,
+             cmp=4 * NT, sg=768, wx=4 * WX, tie=NT + CH, mk=24, hb=512, hx=4 * (CH + NT))),
+    (F, dict(kc=48, jj=24, jx=24, ab=48, jbp=1, ip=1, ip1=1, ip2=1, ip3=1, p16f=1, tha=64, tj=12, t8=4, pl=NT, c96=8, c96a=8,
+             th8=8, c512=1, nab=2, sc=3, dl=3, mt=NT + CH, x0=48, sc0=3, dl0=3, mz=390, scd=3, gd=3, mc=3 * CH, lsb=8,
+             lrow=CH, thr=48, sm=1, dm=1, hrb=4 * CH, hr0=4 * NT, hr1=4 * CH, yb=NT, lir=CH)),
+    (U, dict(z16=8, lst1=6, lin=6, off2=24))) for k, n in names.items()})
+SCRATCH.update(codes(uq=128, ur1=128, t0=NT, vq=512, wq=128, qe=CH + 512, zq=NZ, cq=NT, wxq=WX, xwq=256,
+                     xoq=128, q1=CH, m1=128, big=HO + CH + NT, oq=NT, uin=144, pe=CH + 128))
+SEMAPHORES = ["sV", "sT", "sS", "sG", "du", "dx0", "dx1", "dx2", "dv0", "dv1", "dv2", "dv3", "dw", "dst",
+              "au", "aq", "at", "am", "al", "aa", "go", "go2", "ls"]
 
 OP = AluOpType
 AF = ActivationFunctionType
-BIG1, BIG16, BIG32 = 1.5 * 2.0 ** 23, 1.5 * 2.0 ** 27, 1.5 * 2.0 ** 28
+BIG1, BIG32 = 1.5 * 2.0 ** 23, 1.5 * 2.0 ** 28
 ULP = 1.03125 * 2.0 ** -24
 TINY = 1e-37
+FAR = 1e29
 C05 = 13421773 * 2.0 ** -28
 BANKS = ["b%d" % k for k in range(8)]
+
+ORDER = """
+ubz jj ub xb0 xb1 pp xb2 zbz jx ebz c75 ip ebz2 w23 c96 c96a urb1 uq ip1 zbz2 aba urb2 >au0 hbz q0 urb3 uinz ip2 cmk zu
+t8 ones kc zp2 t00 zo12 zd ebi jbp zp3 zo10 t01 ip3 zo11 zo13 abb p16f nab0 th8 t02 zo01 zt2 urb0 eq1 tri wa z16 eq0
+zo02 zo00 zp0 zo03 zp1 ur2 wx3 >at0 eq2 k12 >at1 xz ur1 ur1s b2 go tha b3 b1 vb0 zq nab1 vb1 tj zt1 vb2 sc b7 vb3 dl b0
+pl b6 cm21 mt2 cm20 sg1 mt1 cm22 sg0 cm10 mt0 cq2 cm12 cm11 cm02 cm00 b4 b4.2 cm01 b1.2 b2.2 cq1 b3.2 b5 cq0 sc0 xs1
+b4.3 dl0 w20 b4.4 b4.5 cm10.2 xl2 b2.3 mz1 x0 w21 wxa wx2 sg2 wx0 wxx sg5 wx1 mz2 xs2 wxq sg3 vq1 cm01.2 b0.2 vq0 zt4
+b0.3 zt5 cm20.2 cm21.2 lst1 b3.3 xl1 eq3 q1s q1 b1.3 b6.2 zt3 cm02.2 >aq0 mz0 vq3 >aq1 hr00 cm22.2 >al0 cm11.2 >aa0
+c512 vq2 zt0 hr01 cm00.2 >aa1 cq2.2 b7.2 xs0 cq0.2 b3.4 go2 zq2 hr02 wb h00 h01 h02 b4.6 b0.4 b1.4 hrb0 b6.3 b7.3 hrb1
+b2.4 hrb2 b4.7 hb0 hrb3 b0.5 hb1 b6.4 lrow hb2 hb3 b1.5 pes b1.6 b1.7 m1 b7.4 st0 hr03 pec b4.8 >am0 wq >am1 gd b2.5
+sg4 thr1 scd h03 cm12.2 lsb mc0 cq1.2 mk mc1 bh0a xl0 xg3 w22 xg0 tie0 xg1 tie1 xg2 tie2 mc2 bh0b xwq tie3 b0.6 b2.6
+b1.8 sm b7.5 dm hr10 cm12.3 mt1.2 cm11.3 b0.7 cm10.3 b4.9 mt0.2 b4.10 cm01.3 mt2.2 b2.7 cm00.3 b6.5 mt3 cq1.3 thr0 thr2
+hr12 cm02.3 thr3 cm03 b4.11 b3.5 h10 b4.12 cq0.3 b5.2 hr11 h12 hr13 b4.13 h11 b1.9 b3.6 xo b3.7 wx0.2 wx1.2 b3.8 xoq
+b3.9 h13 wx2.2 b3.10 bh1 off2 wx3.2 oq0 oqs0 oq1 oqs1 b7.6 st1 oq2 oqs2 b0.8 wxq.2 yb0 yb1 b2.8 st2 b6.6 b6.7 yb2 st3
+st7 lir st8 st9
+"""
 
 
 def sched(g, T):
     eng = {"V": g.vector, "T": g.tensor, "S": g.scalar, "G": g, "Y": g.sync}
     cnt = {"V": 0, "T": 0, "S": 0, "G": 0}
-    wr, rd, seen = {}, {}, {}
+    wr, rd, seen, steps, names = {}, {}, {}, [], {}
 
     def wait(q, reads, writes):
         req = {}
         for k in reads:
-            for qq, s, v in wr.get(k, []):
+            for qq, s, v in wr[k]:
                 req[s] = max(req.get(s, 0), v)
             if k in BANKS:
                 for qq, s, v in rd.get(k, []):
@@ -78,29 +86,33 @@ def sched(g, T):
                 eng[q].wait_ge(T.sem[s], v)
                 seen[(q, s)] = v
 
-    def note(q, s, v, reads, writes):
-        for k in reads:
-            rd.setdefault(k, []).append((q, s, v))
-        for k in writes:
-            wr[k] = [(q, s, v)]
-            rd[k] = []
-
-    def op(q, call, reads, writes):
-        wait(q, reads, writes)
-        cnt[q] += 1
-        call(eng[q]).then_inc(T.sem["s" + q], 1)
-        note(q, "s" + q, cnt[q], reads, writes)
-
-    def dma(q, pairs, s, v, reads, writes):
-        wait(q, reads, writes)
-        for o, i in pairs:
-            eng[q].dma_start(o, i).then_inc(T.sem[s], 16)
-        note("dma", s, v, reads, writes)
+    def step(q, call, reads, writes, sem=None, val=0):
+        k = writes[0]
+        names[k] = names.get(k, 0) + 1
+        steps.append((k if names[k] == 1 else "%s.%d" % (k, names[k]), q, call, list(reads), list(writes), sem, val))
 
     def arrive(s, v, keys):
         for k in keys:
             wr[k] = [("far", s, v)]
-    return op, dma, arrive, wait, cnt
+
+    def issue():
+        by = {s[0]: s for s in steps}
+        for name in (ORDER.split() or [s[0] for s in steps]):
+            _, q, call, reads, writes, sem, val = by.pop(name)
+            wait(q, reads, writes)
+            if sem is None:
+                cnt[q] += 1
+                call(eng[q]).then_inc(T.sem["s" + q], 1)
+                mark = (q, "s" + q, cnt[q])
+            else:
+                call(eng[q])
+                mark = ("dma", sem, val)
+            for k in reads:
+                rd.setdefault(k, []).extend([mark] if sem != "" else [])
+            for k in writes:
+                wr[k], rd[k] = ([mark] if sem != "" else []), []
+        assert not by
+    return step, arrive, issue, cnt, steps
 
 
 def rank_program(g, core, T, topo):
@@ -109,9 +121,19 @@ def rank_program(g, core, T, topo):
         return
     n = len(T.cores)
     nxt, nx2, prv = T.cores[(r + 1) % n], T.cores[(r + 2) % n], T.cores[(r - 1) % n]
-    op, dma, arrive, wait, cnt = sched(g, T)
+    op, arrive, issue, cnt, _ = sched(g, T)
     ps = T.ps
-    loc = [0]
+    loc, sent, stores = [0], [], [0]
+
+    def dma(q, pairs, s, v, reads, writes):
+        def call(e):
+            for o, i in pairs:
+                e.dma_start(o, i).then_inc(T.sem[s], 16)
+        op(q, call, reads, writes, s, v)
+
+    def store(q, pairs, reads):
+        dma(q, pairs, "dst", 0, reads, ["st%d" % stores[0]])
+        stores[0] += len(pairs)
 
     def half(dst, k):
         e = topo.engines(core, dst)
@@ -121,9 +143,10 @@ def rank_program(g, core, T, topo):
         return sum(1 << e for e in es)
 
     def send(dst, out, src, sem, es, reads):
-        wait("G", reads, [])
         rid, pid, _ = topo.addr(dst)
-        g.remote_dma(out, src, T.sem[sem], T.sem["ls"], pid, rid, bits(es))
+        k = ">" + sem + str(len([x for x in sent if x[1:3] == sem]))
+        sent.append(k)
+        op("G", lambda e: e.remote_dma(out, src, T.sem[sem], T.sem["ls"], pid, rid, bits(es)), reads, [k], "")
         loc[0] += len(es)
 
     def u8(name, a, b):
@@ -134,57 +157,70 @@ def rank_program(g, core, T, topo):
     arrive("at", 32, ["bt"])
     arrive("am", 32, ["bm"])
     arrive("al", 8, ["lin"])
-    arrive("ao", 8, ["offd"])
-    arrive("go", 1, ["go"])
-    arrive("go2", 1, ["go2"])
+    arrive("aa", 16, ["za"])
+
+    def keys(k):
+        return [k] if isinstance(k, str) else k
 
     def V(f, reads, writes):
-        op("V", f, reads, writes)
+        op("V", f, reads, keys(writes))
 
     def S(f, reads, writes):
-        op("S", f, reads, writes)
+        op("S", f, reads, keys(writes))
 
     def G(f, reads, writes):
-        op("G", f, reads, writes)
+        op("G", f, reads, keys(writes))
 
     def memset(ap, c, key, after=()):
-        V(lambda e: e.memset(ap, c), list(after), [key])
+        V(lambda e: e.memset(ap, c), list(after), key)
 
-    def iota(ap, pattern, key, cm=0, base=0):
-        G(lambda e: e.iota(ap, pattern, base, cm, allow_small_or_imprecise_dtypes=True), [], [key])
+    def iota(ap, pattern, key, cm=0, base=0, after=()):
+        G(lambda e: e.iota(ap, pattern, base, cm, allow_small_or_imprecise_dtypes=True), list(after), key)
+
+    def asel(out, in_, pattern, o, fill, base, cm, reads, key):
+        G(lambda e: e.affine_select(out, in_, pattern, o, fill, base, cm), reads, key)
 
     def ts(out, in0, s1, o, reads, key):
-        V(lambda e: e.tensor_scalar(out, in0, s1, None, o), reads, [key])
+        V(lambda e: e.tensor_scalar(out, in0, s1, None, o), reads, key)
+
+    def ts2(out, in0, s1, o1, s2, o2, reads, key):
+        V(lambda e: e.tensor_scalar(out, in0, s1, s2, o1, o2), reads, key)
 
     def tt(out, in0, in1, o, reads, key):
-        V(lambda e: e.tensor_tensor(out, in0, in1, o), reads, [key])
+        V(lambda e: e.tensor_tensor(out, in0, in1, o), reads, key)
 
     def cp(out, in_, reads, key):
-        V(lambda e: e.tensor_copy(out, in_), reads, [key])
+        V(lambda e: e.tensor_copy(out, in_), reads, key)
 
     def act(out, in_, f, bias, scale, reads, key):
-        S(lambda e: e.activation(out, in_, f, bias=bias, scale=scale), reads, [key])
+        S(lambda e: e.activation(out, in_, f, bias=bias, scale=scale), reads, key)
+
+    def zeros(w):
+        return T.ub[:, 8:8 + w]
+
+    def ones(w):
+        return T.ub[:, ONE:ONE + w]
 
     def zero(out, w, key):
-        S(lambda e: e.activation(out, T.ub[:, 8:8 + w], AF.Copy), ["ubz"], [key])
+        S(lambda e: e.activation(out, zeros(w), AF.Copy), ["ubz"], key)
 
     def quant(out, a, b, src, reads, key):
-        V(lambda e: e.quantize_mx(T[out][:, a:b], T[out + "s"][:, a:b], src), reads, [key])
+        V(lambda e: e.quantize_mx(T[out][:, a:b], T[out + "s"][:, a:b], src), reads, key)
 
     def mm(bank, w, L, l0, R, r0, start, stop, reads):
         op("T", lambda e: e.matmul_mx(ps[:, 512 * bank:512 * bank + w], T[L][:, l0:l0 + 128], T[L + "s"][:, l0:l0 + 128],
                                       T[R][:, r0:r0 + w], T[R + "s"][:, r0:r0 + w], start, stop), reads, ["b%d" % bank])
 
-    def B(bank, a, b):
-        return ps[:, 512 * bank + a:512 * bank + b]
+    def B(bank, a, b, s=1):
+        return ps[:, 512 * bank + a:512 * bank + b:s]
 
     def pick_c(dst, d0, w, src, a, b, off, o0, reads, key):
         V(lambda e: e.tensor_copy(T[dst][:, d0:d0 + w].bitcast(dt.uint32),
-                                  T[src][:, a:b].bitcast(dt.uint32).indirect(T[off][:, o0:o0 + w // 16])), reads, [key])
+                                  T[src][:, a:b].bitcast(dt.uint32).indirect(T[off][:, o0:o0 + w // 16])), reads, key)
 
     def pick_s(dst, d0, w, src, a, b, off, o0, reads, key):
         S(lambda e: e.activation(T[dst + "s"][:, d0:d0 + w], T[src + "s"][:, a:b].indirect(T[off][:, o0:o0 + w // 16]),
-                                 AF.Copy), reads, [key])
+                                 AF.Copy), reads, key)
 
     def hk(key, k=4):
         return [key + str(i) for i in range(k)]
@@ -194,106 +230,119 @@ def rank_program(g, core, T, topo):
         dma("Y", [(T.xb[:, 512 * c:512 * c + 512], T.x[:, 512 * c:512 * c + 512])], "dx%d" % c, 16, [], ["xb%d" % c])
 
     memset(T.ub[:, 8:512], 0.0, "ubz")
-    memset(T.ones[:], 1.0, "ones")
+    memset(ones(256), 1.0, "ones")
     iota(T.jj[:], [[0, 6], [128, 4]], "jj", 1)
     iota(T.ip[:], [[0, 1]], "ip", 2)
-    G(lambda e: e.affine_select(T.c75[:], T.ub[:, 8:9], [[1, 1]], OP.not_equal, -7.5, 0, 1), ["ubz"], ["c75"])
+    asel(T.c75[:], zeros(1), [[1, 1]], OP.not_equal, -7.5, 0, 1, ["ubz"], "c75")
     iota(T.q0[:], [[0, 8], [1, 16]], "q0")
-    quant("uq", 0, 128, T.ub[:], ["ub", "ubz"], "uq")
-    memset(T.zb[:], 0.0, "zbz")
     memset(T.z16[:], 0, "z16")
+    memset(T.zb[:, 0:4 * ZA], 0.0, "zbz")
+    quant("uq", 0, 128, T.ub[:, 0:512], ["ub", "ubz"], "uq")
     quant("uin", 0, 128, T.zb[:, 0:512], ["zbz"], "uinz")
-    wait("G", ["uq"], [])
     rid, pid, _ = topo.addr(prv)
     e0 = half(prv, 0)
-    g.remote_dma_fused([RemoteDMATransfer(dst_ids=[DstId(rid=rid, pnc=pid)], dma_engine_mask=bits(e0[:4]), remote_sem=T.sem["au"],
-                                          src=u8("uq", 0, 2), dst=u8("uin", 128, 130)),
-                        RemoteDMATransfer(dst_ids=[DstId(rid=rid, pnc=pid)], dma_engine_mask=bits(e0[4:]), remote_sem=T.sem["au"],
-                                          src=T.uqs[:, 0:8], dst=T.uins[:, 128:136])], local_sem=T.sem["ls"])
+    op("G", lambda e: e.remote_dma_fused(
+        [RemoteDMATransfer(dst_ids=[DstId(rid=rid, pnc=pid)], dma_engine_mask=bits(e0[:4]), remote_sem=T.sem["au"],
+                           src=u8("uq", 0, 2), dst=u8("uin", 128, 130)),
+         RemoteDMATransfer(dst_ids=[DstId(rid=rid, pnc=pid)], dma_engine_mask=bits(e0[4:]), remote_sem=T.sem["au"],
+                           src=T.uqs[:, 0:8], dst=T.uins[:, 128:136])], local_sem=T.sem["ls"]), ["uq"], [">au0"], "")
     loc[0] += len(e0)
     zero(T.eb[:, 0:504], 504, "ebz")
     zero(T.eb[:, 504:520], 16, "ebz2")
-    G(lambda e: e.affine_select(T.eb[:, 4:516:4], T.ones[:], [[-1, 128]], OP.is_equal, 0.0, 0, 1), ["ones", "ebz", "ebz2"], ["ebi"])
-    G(lambda e: e.affine_select(T.tri[:], T.ones[:], [[1, 128]], OP.is_gt, 0.0, 0, -1), ["ones"], ["tri"])
+    asel(T.eb[:, 4:516:4], ones(128), [[-1, 128]], OP.is_equal, 0.0, 0, 1, ["ones", "ebz", "ebz2"], "ebi")
+    asel(T.ub[:, TRI:ONE], ones(128), [[1, 128]], OP.is_gt, 0.0, 0, -1, ["ones"], "tri")
     iota(T.kc[:], [[0, 2], [16, 6], [0, 4]], "kc")
-    iota(T.pp[:], [[1, 128]], "pp")
-    iota(T.j96[:], [[128, 4]], "j96", 1, CH)
+    iota(T.tha[:], [[0, 8], [1000, 2], [0, 4]], "tha", 0, CH)
     act(T.jx[:], T.jj[:], AF.Identity, BIG32, 1.0, ["jj"], "jx")
     act(T.ip1[:], T.ip[:], AF.Identity, -15.0, 1.0, ["ip"], "ip1")
     act(T.ab[:, 0:24], T.jx[:], AF.Identity, -BIG32, 1.0, ["jx"], "aba")
     act(T.ip2[:], T.ip1[:], AF.Identity, BIG1, 1.0 / 32, ["ip1"], "ip2")
     act(T.jbp[:], T.ab[:, 0:1], AF.Identity, T.jj[:, 0:1], -1.0, ["aba", "jj"], "jbp")
     act(T.ip3[:], T.ip2[:], AF.Identity, -BIG1, 1.0, ["ip2"], "ip3")
-    act(T.ab[:, 24:48], T.ub[:, 8:32], AF.Identity, T.jbp[:, 0:1], 1.0, ["ubz", "jbp"], "abb")
-    act(T.cmp[:, 3:4 * NT:4], T.ub[:, 8:8 + NT], AF.Identity, T.c75[:, 0:1], 1.0, ["ubz", "c75"], "cmk")
+    act(T.ab[:, 24:48], zeros(24), AF.Identity, T.jbp[:, 0:1], 1.0, ["ubz", "jbp"], "abb")
+    act(T.cmp[:, 3:4 * NT:4], zeros(NT), AF.Identity, T.c75[:, 0:1], 1.0, ["ubz", "c75"], ["cmk", "cm03"])
     act(T.p16f[:], T.ip3[:], AF.Identity, T.jj[:, 0:1], -16.0, ["ip3", "jj"], "p16f")
-    zero(T.wx[:, 51:560:4], 128, "wxz")
-    act(T.qm[:], T.q0[:], AF.Identity, -7.5, 1.0, ["q0"], "qm")
+    zero(T.wx[:, 51:560:4], 128, "wx3")
     for t in range(4):
         for a in range(2):
-            k = 24 if t < 3 else 12
-            act(T.zb[:, 388 * a + 8 + t:388 * a + 8 + 16 * k:16], T.ones[:, 0:k], AF.Copy, 0.0, 1.0, ["ones", "zbz", "uinz"], "zo%d%d" % (a, t))
-    act(T.zb[:, 888:891], T.ub[:, 8:11], AF.Identity, T.jbp[:, 0:1], 1.0, ["ubz", "jbp", "zbz"], "zba")
-    act(T.zb[:, 896:899], T.ab[:, 0:3], AF.Copy, 0.0, 1.0, ["aba", "zbz"], "zbb")
+            k = 17 if t < 3 else 16
+            b = (8, 4 * ZO + 4)[a]
+            act(T.zb[:, b + t:b + 16 * k:16], ones(k), AF.Copy, 0.0, 1.0, ["ones", "zbz", "uinz"], "zo%d%d" % (a, t))
+    memset(T.zb[0:1, 4 * ZU + 3:4 * ZU + 256:4], -2.0 ** 25, "zu", ["zbz", "uinz"])
+    memset(T.zb[0:1, 4 * ZD + 3:4 * ZD + 256:4], 2.0 ** 25, "zd", ["zbz", "uinz"])
+    for t in range(4):
+        act(T.urb[:, t:512:4], zeros(128), AF.Identity, T.ub[:, t:t + 1], 1.0, ["ub", "ubz"], "urb%d" % t)
+    zero(T.hb[:, 4 * CH:512], 128, "hbz")
+    act(T.wa[:], T.q0[:], AF.Abs, T.p16f[:, 0:1], -1.0, ["q0", "p16f"], "wa")
+    zero(T.xw[:, 515:1024:4], 128, "w23")
 
     def EQ(b):
         quant("qe", CH + 128 * b, CH + 128 * b + 128, T.eb[:, 4 - b:516 - b], ["ebz", "ebz2", "ebi"], "eq%d" % b)
     for c in range(3):
         quant("t0", 128 * c, 128 * c + 128, T.xb[:, 512 * c:512 * c + 512], ["xb%d" % c], "t0%d" % c)
-        if c < 2:
-            EQ(c)
+    for b in range(4):
+        EQ(b)
     t0 = hk("t0", 3)
-    send(nx2, u8("big", T0, T0 + NT), u8("t0", 0, NT), "at", topo.engines(core, nx2), t0)
-    send(nx2, T.bigs[:, T0:T0 + NT], T.t0s[:, 0:NT], "at", topo.engines(core, nx2), [])
-    g.sem_inc(T.sem["go"], 1)
+    send(nx2, u8("big", CH, CH + NT), u8("t0", 0, NT), "at", topo.engines(core, nx2), t0)
+    send(nx2, T.bigs[:, CH:CH + NT], T.t0s[:, 0:NT], "at", topo.engines(core, nx2), t0)
+    op("G", lambda e: e.sem_inc(T.sem["go"], 1), [">at0", ">at1"], ["go"], "go", 1)
     for i in range(4):
         dma("Y", [(T.vb[:, 512 * i:512 * i + 512], T.v[:, 512 * i:512 * i + 512])], "dv%d" % i, 16, ["go", "uin"], ["vb%d" % i])
+    iota(T.tj[:], [[-128, 3], [128, 4]], "tj")
+    iota(T.t8[:], [[8, 4]], "t8", 0, -12)
+    iota(T.xw[:, 0:512], [[0, 512]], "xz")
+    iota(T.pp[:], [[1, 128]], "pp")
+    iota(T.xw[0:32, 1:96:4], [[16, 24]], "xs0", 0, -192, ["xz"])
+    memset(T.xw[32:64, 1:96:4], 192.0 + CH, "xs1", ["xz"])
+    iota(T.c96[:], [[0, 8]], "c96", 0, CH)
+    iota(T.k12[:], [[1, 24]], "k12", 0, -12)
+    asel(T.c96a[:], T.c96[:], [[-16, 8]], OP.is_ge, 0.0, 0, 1, ["c96"], "c96a")
+    asel(T.c512[:], zeros(1), [[1, 1]], OP.is_ge, float(HO), -CH, 1, ["ubz"], "c512")
+    asel(T.th8[:], T.c96a[:], [[16, 8]], OP.is_ge, 0.0, 15, -1, ["c96a"], "th8")
+    iota(T.pl[:], [[1, NT]], "pl")
+    memset(T.zb[:, 4 * ZB:4 * NZ], 0.0, "zbz2")
+    for t in range(3):
+        memset(T.zb[0:CH, 4 * ZP + 65 * t:4 * ZP + 64 * t + 64:8], 1.0, "zp%d" % t, ["zbz2"])
+    memset(T.zb[0:CH, 4 * ZP + 7:4 * ZP + 192:8], 1.0, "zp3", ["zbz2"])
+    quant("zq", 0, ZA, T.zb[:, 0:4 * ZA], ["zbz", "zu", "zd"] + hk("zo0") + hk("zo1"), "zq")
+    quant("pe", CH, CH + 128, T.urb[:], hk("urb"), "ur2")
 
     ROW = (0, 6, 7)
     SC = 126
 
-    def col(c, tok, ur, keys, at=0):
-        mm(1 + c, 128, tok, 128 * c, ur, at, True, True, keys)
-
-    def row(c, tok, ur, keys):
-        mm(ROW[c], 128, ur, 0, tok, 128 * c, True, True, keys)
-
-    def slot(c, t):
-        return T.cmp[:, 512 * c + t:512 * c + 512:4]
+    def slot(c, t, w=128):
+        return T.cmp[:, 512 * c + t:512 * c + 4 * w:4]
 
     def against(c, t):
         if c == t:
             tt(slot(c, c), B(ROW[c], 0, 128), T.mt[:, 128 * c:128 * c + 128], OP.is_lt, ["b%d" % ROW[c], "mt%d" % c], "cm%d%d" % (c, c))
         else:
-            ts(slot(c, t), B(ROW[c], 0, 128), T.sc[:, t:t + 1], OP.is_le if t < c else OP.is_lt, ["b%d" % ROW[c], "sc%d" % t], "cm%d%d" % (c, t))
+            ts(slot(c, t), B(ROW[c], 0, 128), T.sc[:, t:t + 1], OP.is_le if t < c else OP.is_lt, ["b%d" % ROW[c], "sc"], "cm%d%d" % (c, t))
 
     def sign(c, t):
-        k = c + t - 1
-        act(T.sg[:, 128 * k:128 * k + 128], B(ROW[c], 0, 128), AF.Sign, T.sc[:, t:t + 1], -1.0, ["b%d" % ROW[c], "sc%d" % t], "sg%d" % k)
+        act(T.sg[:, 128 * c:128 * c + 128], B(ROW[c], 0, 128), AF.Sign, T.sc[:, t:t + 1], -1.0, ["b%d" % ROW[c], "sc"], "sg%d" % c)
 
-    def relu(c, t):
-        k = c + t - 1
+    def relu(c, t, k):
         act(slot(c, t), T.sg[:, 128 * k:128 * k + 128], AF.Relu, 0.0, 1.0, ["sg%d" % k], "cm%d%d" % (c, t))
 
-    def score(a, b):
-        S(lambda e: e.activation(T.sc[:, a:b], ps[:, 512 * a + 512 + SC:512 * b + 512:512], AF.Copy),
-          ["b%d" % (1 + c) for c in range(a, b)], ["sc%d" % c for c in range(a, b)])
-
-    def step(a, b):
-        S(lambda e: e.activation(T.dl[:, a:b], ps[:, 512 * a + 512 + SC:512 * b + 512:512], AF.Abs, bias=TINY, scale=ULP),
-          ["b%d" % (1 + c) for c in range(a, b)], ["dl%d" % c for c in range(a, b)])
+    def score(sc, dl, at):
+        cols = ps[:, 512 + at:2048:512]
+        act(T[sc][:], cols, AF.Copy, 0.0, 1.0, ["b1", "b2", "b3"], sc)
+        act(T[dl][:], cols, AF.Abs, TINY, ULP, ["b1", "b2", "b3"], dl)
 
     def shift(c):
-        act(T.mt[:, 128 * c:128 * c + 128], T.tri[:], AF.Identity, T.sc[:, c:c + 1], T.dl[:, c:c + 1], ["tri", "sc%d" % c, "dl%d" % c], "mt%d" % c)
+        act(T.mt[:, 128 * c:128 * c + 128], T.ub[:, TRI:ONE], AF.Identity, T.sc[:, c:c + 1], T.dl[:, c:c + 1], ["tri", "sc", "dl"], "mt%d" % c)
 
-    def pack(c):
-        quant("cq", 128 * c, 128 * c + 128, T.cmp[:, 512 * c:512 * c + 512], hk("cm%d" % c, 3) + ["cmk"], "cq%d" % c)
+    def pack(c, more=()):
+        quant("cq", 128 * c, 128 * c + 128, T.cmp[:, 512 * c:512 * c + 512], hk("cm%d" % c, 3) + ["cmk"] + list(more), "cq%d" % c)
 
     def position(c):
-        mm(4, 128, "cq", 128 * c, "zq", (2, 98, 0)[c], c == 2, c == 0, ["cq%d" % c, "zq"])
+        mm(4, 128, "cq", 128 * c, "zq", (2, ZO, 0)[c], False, False, ["cq%d" % c, "zq"])
 
-    def R(i, bank, q, q0, w, out, w2, keys):
+    def Rm(i, bank, q, q0, w, keys):
         mm(bank, w, "vq", 128 * i, q, q0, True, True, keys + ["vq%d" % i])
+
+    def Ra(i, bank, out, w2):
         act(T[out][:, w2 * i:w2 * i + w2], B(bank, 0, w2), AF.Relu, 0.0, C05, ["b%d" % bank], out + str(i))
 
     def D(i, bank, q, q0, w, keys):
@@ -302,170 +351,204 @@ def rank_program(g, core, T, topo):
     def add(i, bank, h, c0, w, hr, key):
         tt(T[h][:, 4 * c0 + i:4 * (c0 + w):4], T[hr][:, w * i:w * i + w], B(bank, 0, w), OP.add, [hr + str(i), "b%d" % bank], key + str(i))
 
-    def D0(b):
-        D(b, b, "big", T0, NT, ["bt"])
+    def D0(i, bank):
+        D(i, bank, "big", CH, NT, ["bt"])
 
     def R0(i, bank):
-        R(i, bank, "big", T0, NT, "hr0", NT, ["bt"])
+        Rm(i, bank, "big", CH, NT, ["bt"])
+        Ra(i, bank, "hr0", NT)
 
-    def A0(i):
-        add(i, i, "hx", CH, NT, "hr0", "h0")
+    def A0(i, bank):
+        add(i, bank, "hx", CH, NT, "hr0", "h0")
 
     def VQ(i):
         quant("vq", 128 * i, 128 * i + 128, T.vb[:, 512 * i:512 * i + 512], ["vb%d" % i], "vq%d" % i)
 
     uk = ["uin", "uinz"]
-    EQ(2)
     for c in range(3):
-        col(c, "t0", "uin", ["t0%d" % c] + uk, 2)
+        mm(1 + c, 128, "t0", 128 * c, "uin", 2, True, True, ["t0%d" % c] + uk)
     pick_s("ur1", 0, 128, "uin", 128, 130, "z16", 0, uk + ["z16"], "ur1s")
     pick_c("ur1", 0, 128, "uin", 128, 130, "z16", 0, uk + ["z16"], "ur1")
     for c in (2, 0, 1):
-        row(c, "t0", "ur1", ["t0%d" % c, "ur1", "ur1s"])
-    quant("zq", 0, NZ, T.zb[:], ["zbz", "zba", "zbb"] + hk("zo0") + hk("zo1"), "zq")
-    score(0, 3), step(0, 3), shift(2), sign(0, 2), sign(1, 2), shift(1), shift(0), relu(1, 2), relu(0, 2)
+        mm(ROW[c], 128, "ur1", 0, "t0", 128 * c, True, True, ["t0%d" % c, "ur1", "ur1s"])
+    score("sc", "dl", SC), shift(2), sign(0, 2), sign(1, 2), shift(1), shift(0), relu(1, 2, 1), relu(0, 2, 0)
     for c, t in ((2, 0), (2, 1), (2, 2), (0, 1), (1, 0), (1, 1)):
         against(c, t)
     pack(2), against(0, 0), pack(1), pack(0)
+    mm(4, 128, "cq", 256, "zq", ZU, True, False, ["cq2", "zq"])
     position(2), position(1), position(0)
-    D0(0)
-    for t in range(4):
-        act(T.urb[:, t:512:4], T.ub[:, 8:136], AF.Identity, T.ub[:, t:t + 1], 1.0, ["ub", "ubz"], "urb%d" % t)
-    act(T.wa[:], T.q0[:], AF.Abs, T.p16f[:, 0:1], -1.0, ["q0", "p16f"], "wa")
-    act(T.c88[:, 0:48], T.ones[:, 0:48], AF.Identity, CH - 9.0, 1.0, ["ones"], "c88a")
-    act(T.c88[:, 48:96], T.ones[:, 0:48], AF.Identity, CH - 1.5, 1.0, ["ones"], "c88b")
-    zero(T.hb[:, 4 * CH:512], 128, "hbz")
-    zero(T.xo[:, 96:512], 416, "xoz")
-    V(lambda e: e.tensor_scalar(T.kl[:], B(4, 0, 48), BIG16, BIG16, OP.add, OP.subtract), ["b4"], ["kl"])
-    V(lambda e: e.tensor_scalar(T.ak[:], B(4, 48, 52), CH - 0.5, 1000.0, OP.subtract, OP.mult), ["b4"], ["ak"])
-
-    def offn(t):
-        V(lambda e: e.tensor_scalar(T.offn[:, t:t + 1], B(4, 48 + t, 49 + t), T.ak[:, t:t + 1], T.j96[:, t:t + 1], OP.max, OP.min),
-          ["b4", "ak", "j96"], ["offn%d" % t])
-    tt(T.x0[:], T.kl[:], T.kc[:], OP.is_equal, ["kl", "kc"], "x0")
+    mm(4, 128, "cq", 0, "zq", ZD, False, True, ["cq0", "zq"])
+    for c in range(3):
+        mm(1 + c, 128, "big", CH + 128 * c, "pe", CH, True, True, ["bt", "ur2"])
+    mm(5, NT, "pe", CH, "big", CH, True, True, ["bt", "ur2"])
+    zt = 4 * ZT
+    act(T.zb[:, zt:zt + 12], T.tj[:], AF.Identity, T.ab[:, 0:1], 1.0, ["tj", "aba", "zbz2"], "zt0")
+    act(T.zb[:, zt + 12:zt + 16], T.ab[:, 24:28], AF.Copy, 0.0, 1.0, ["abb", "zbz2"], "zt1")
+    act(T.zb[:, zt + 16:zt + 20], T.t8[:], AF.Identity, T.ip3[:, 0:1], 1.0, ["t8", "ip3", "zbz2"], "zt2")
+    act(T.zb[:, zt + 20:zt + 24], zeros(4), AF.Identity, T.p16f[:, 0:1], 1.0, ["ubz", "p16f", "zbz2"], "zt3")
+    act(T.zb[:, zt + 24:zt + 28], T.ab[:, 0:4], AF.Copy, 0.0, -1.0 / HO, ["aba", "zbz2"], "zt4")
+    act(T.zb[:, zt + 28:zt + 32], T.ab[:, 24:28], AF.Copy, 0.0, -1.0 / HO, ["abb", "zbz2"], "zt5")
+    act(T.xw[:, 512:1024:4], T.wa[:], AF.Relu, float(HO), -float(HO), ["wa"], "w20")
+    act(T.xw[:, 513:1024:4], T.wa[:], AF.Relu, 0.5, -0.5, ["wa"], "w21")
+    act(T.nab[:, 0:1], T.ab[:, 0:1], AF.Identity, -CH / HO, 1.0 / HO, ["aba"], "nab0")
+    act(T.nab[:, 1:2], T.jbp[:], AF.Copy, 0.0, 1.0 / HO, ["jbp"], "nab1")
+    act(T.xw[:, 480:483], T.ab[:, 0:3], AF.Copy, 0.0, 1.0, ["aba", "xz"], "xl1")
+    act(T.xw[:, 488:491], T.ab[:, 24:27], AF.Copy, 0.0, 1.0, ["abb", "xz"], "xl2")
+    act(T.xw[64:96, 1:96:4], T.ub[64:96, 8:32], AF.Identity, T.p16f[64:96, 0:1], 1.0, ["ubz", "p16f", "xz"], "xs2")
+    score("sc0", "dl0", 0)
+    for c in range(3):
+        act(T.mz[:, 130 * c:130 * c + 129], T.ub[:, TRI:ONE + 1], AF.Identity, T.sc0[:, c:c + 1], T.dl0[:, c:c + 1],
+            ["tri", "ones", "sc0", "dl0"], "mz%d" % c)
+    tt(T.wx[:, 560:560 + 4 * NA], T.tha[:], B(4, 0, 4 * NA), OP.is_le, ["tha", "b4"], "wxa")
+    tt(T.x0[:], B(4, 0, 48), T.kc[:], OP.is_equal, ["b4", "kc"], "x0")
     for t in range(3):
-        V(lambda e, t=t: e.tensor_scalar(T.wx[:, 48 + t:560:4], T.qm[:], T.kl[:, t:t + 1], B(4, t, t + 1), OP.add, OP.is_equal),
-          ["kl", "qm", "b4"], ["wx%d" % t])
-        if t == 1:
-            tt(T.wx[:, 0:48], T.x0[:], T.ab[:], OP.mult, ["x0", "aba", "abb"], "wxx")
-    offn(0)
-    quant("wxq", 0, 140, T.wx[:], ["wxz", "wx0", "wx1", "wx2", "wxx"], "wxq")
-    mm(5, 128, "wxq", 12, "wxq", 0, True, False, ["wxq"])
-    mm(5, 128, "wxq", 12, "wxq", 6, False, True, ["wxq"])
-    D0(1)
-    offn(1), offn(2), EQ(3)
-    dma("Y", [(T.offs[k:128:8, :], T.offn[16 * k:16 * k + 16, :]) for k in range(8)], "dof", 128, hk("offn", 3), ["offs"])
-    dma("Y", [(T.wb[:], T.w[:])], "dw", 16, ["go2"], ["wb"])
-    cp(T.lst1[:], B(5, 0, 6), ["b5"], "lst1")
+        ts2(T.wx[:, 48 + t:560:4], T.q0[:], B(4, t, t + 1), OP.add, B(4, 64 + t, 65 + t), OP.is_equal, ["q0", "b4"], "wx%d" % t)
+    tt(T.wx[:, 0:48], T.x0[:], T.ab[:], OP.mult, ["x0", "aba", "abb"], "wxx")
+    quant("wxq", 0, WX, T.wx[:], hk("wx") + ["wxx", "wxa"], ["wxq", "wxqa"])
+    mm(0, 128, "wxq", 12, "wxq", 0, True, False, ["wxq"])
+    mm(0, 128, "wxq", 12, "wxq", 6, False, True, ["wxq"])
+    D0(0, 1), D0(1, 2)
+    quant("zq", ZB, NZ, T.zb[:, 4 * ZB:4 * NZ], ["zbz2"] + hk("zp") + hk("zt", 6), "zq2")
+    cp(T.lst1[:], B(0, 0, 6), ["b0"], "lst1")
     pick_s("q1", 0, CH, "t0", 0, NT, "lst1", 0, t0 + ["lst1"], "q1s")
     pick_c("q1", 0, CH, "t0", 0, NT, "lst1", 0, t0 + ["lst1"], "q1")
     send(nxt, u8("qe", 0, CH), u8("q1", 0, CH), "aq", topo.engines(core, nxt), ["q1"])
     send(nxt, T.qes[:, 0:CH], T.q1s[:, 0:CH], "aq", topo.engines(core, nxt), ["q1s"])
-    g.sem_inc(T.sem["go2"], 1)
     send(nx2, T.lin[:], T.lst1[:], "al", half(nx2, 0), ["lst1"])
-    send(nx2, T.offd[:], T.offs[:], "ao", half(nx2, 0), ["offs"])
-    VQ(0), VQ(1), VQ(2), VQ(3)
-    for t in range(4):
-        act(T.w2b[:, t:512:4], T.wa[:], AF.Relu, float(HALF), -float(HALF), ["wa"], "w2b%d" % t)
-    R0(0, 7), R0(1, 6), R0(2, 2)
-    quant("ur2", 0, 128, T.urb[:], hk("urb"), "ur2")
-    quant("w2", 0, 128, T.w2b[:], hk("w2b"), "w2")
-    A0(0)
-    G(lambda e: e.affine_select(T.tha[:], T.c88[:], [[-16, 24], [128, 4]], OP.is_ge, CH + 392.5, 0, 1), ["c88a", "c88b"], ["tha"])
-    G(lambda e: e.affine_select(T.thr[:], T.tha[:], [[16, 24], [-128, 4]], OP.is_ge, CH + 392.5, 15, -1), ["tha"], ["thr"])
+    send(nx2, u8("zq", ZA, ZA + NA), u8("wxq", 140, WX), "aa", half(nx2, 1), ["wxqa"])
+    send(nx2, T.zqs[:, ZA:ZA + NA], T.wxqs[:, 140:WX], "aa", half(nx2, 0), ["wxqa"])
+    op("G", lambda e: e.sem_inc(T.sem["go2"], 1), [">aq0", ">aq1"], ["go2"], "go2", 1)
+    dma("Y", [(T.wb[:], T.w[:])], "dw", 16, ["go2"], ["wb"])
+    for i in range(4):
+        VQ(i)
 
-    def RB(i, bank):
-        R(i, bank, "qe", 0, 128, "hrb", CH, ["qin", "eq0"])
+    for c in (1, 2):
+        ts(slot(c, 0), B(5, 128 * c, 128 * c + 128), T.sc0[:, 0:1], OP.is_le, ["b5", "sc0"], "cm%d0" % c)
+    for k, (c, t) in ((2, (0, 1)), (3, (0, 2)), (4, (1, 2)), (5, (2, 1))):
+        bias = T.mz[:, 130 * t + 128:130 * t + 129] if t < c else T.sc0[:, t:t + 1]
+        act(T.sg[:, 128 * k:128 * k + 128], B(5, 128 * c, 128 * c + 128), AF.Sign, bias, -1.0, ["b5", "sc0", "mz%d" % t], "sg%d" % k)
+        relu(c, t, k)
+    R0(0, 3), R0(1, 6), R0(2, 7)
+    for c in range(3):
+        tt(slot(c, c), B(5, 128 * c, 128 * c + 128), T.mz[:, 130 * c:130 * c + 128], OP.is_lt, ["b5", "mz%d" % c], "cm%d%d" % (c, c))
+    pack(0), pack(1), pack(2)
+    D0(2, 3)
+    A0(0, 1), A0(1, 2), A0(2, 3)
 
-    def DB(i, bank):
-        D(i, bank, "qe", 0, 128, ["qin", "eq0"])
-
-    def AB(i, bank):
-        add(i, bank, "hb", 0, CH, "hrb", "hb")
-    A0(1)
-    RB(0, 4), RB(1, 5), RB(2, 3), RB(3, 6), DB(0, 7), DB(1, 4), DB(2, 5), DB(3, 3)
-    AB(0, 7), AB(1, 4), AB(2, 5), AB(3, 3)
+    RB, DB = (4, 0, 6, 7), (1, 2, 4, 0)
+    for i in range(4):
+        Rm(i, RB[i], "qe", 0, 128, ["qin", "eq0"])
+        Ra(i, RB[i], "hrb", CH)
+    for i in range(4):
+        D(i, DB[i], "qe", 0, 128, ["qin", "eq0"])
+    for i in range(4):
+        add(i, DB[i], "hb", 0, CH, "hrb", "hb")
     quant("m1", 0, 128, T.hb[:], ["hbz"] + hk("hb"), "m1")
-    send(nxt, u8("big", HALF, HALF + CH), u8("m1", 0, CH), "am", topo.engines(core, nxt), ["m1"])
-    send(nxt, T.bigs[:, HALF:HALF + CH], T.m1s[:, 0:CH], "am", topo.engines(core, nxt), [])
-    dma("Y", [(T.off1a[16 * h:16 * h + 16, :], T.offd[:]) for h in range(8)], "doff", 128, ["offd"], ["off1a"])
-    R0(3, 6), D0(2), D0(3)
-    act(T.pm[:], T.pp[:], AF.Identity, -7.5, 1.0, ["pp"], "pm")
-    quant("wq", 0, 128, T.wb[:], ["wb"], "wq")
-    A0(2)
-    A0(3)
-    quant("big", CH + 192, HALF, T.hx[:, 4 * CH + 768:4 * HALF], hk("h0"), "bh0b")
-    for t in range(3):
-        cp(T.off1[:, 8 * t:8 * t + 8], T.off1a[:, t:24:3], ["off1a"], "off1%d" % t)
-    stores = [0]
+    send(nxt, u8("big", 0, CH), u8("m1", 0, CH), "am", topo.engines(core, nxt), ["m1"])
+    send(nxt, T.bigs[:, 0:CH], T.m1s[:, 0:CH], "am", topo.engines(core, nxt), ["m1"])
 
-    def store(q, pairs, reads):
-        dma(q, pairs, "dst", 0, reads, [])
-        stores[0] += 16 * len(pairs)
+    zk = ["zq", "zq2", "za"]
+    ek = hk("eq", 3) + ["lin"]
+    pick_s("pe", 0, CH, "qe", CH, CH + NT, "lin", 0, ek, "pes")
+    pick_c("pe", 0, CH, "qe", CH, CH + NT, "lin", 0, ek, "pec")
+    S(lambda e: e.activation(T.lrow[:], T.pl[:].indirect(T.lin[:]), AF.Copy), ["pl", "lin"], "lrow")
+    R0(3, 6), D0(3, 7)
+    for t in range(3):
+        mm(1, 128, "qe", CH + 128 * t, "zq", ZA - 16 * t, t == 0, t == 2, zk + ["eq%d" % t])
+    mm(2, 128, "pe", 0, "zq", ZA, True, True, zk + ["pes", "pec", "ur2"])
+    for c in range(3):
+        mm(4, 128, "cq", 128 * c, "zq", ZA - 16 * c, c == 0, False, zk + ["cq%d" % c])
+    act(T.lsb[:], B(2, ZT - ZA, ZT - ZA + 8), AF.Copy, 0.0, 1.0, ["b2"], "lsb")
+    act(T.gd[:], B(1, 0, 48, 16), AF.Identity, -FAR, FAR, ["b1"], "gd")
+    quant("wq", 0, 128, T.wb[:], ["wb"], "wq")
+    A0(3, 7)
+
+    def L(i):
+        return T.lsb[:, i:i + 1]
+    tt(T.scd[:], T.sc0[:], T.gd[:], OP.add, ["sc0", "gd"], "scd")
+    ts(T.mk[:], T.k12[:], L(4), OP.is_equal, ["k12", "lsb"], "mk")
+    for t in range(3):
+        ts2(T.tie[:, 128 * t:128 * t + 128], T.pp[:], L(3), OP.subtract, L(t), OP.is_gt, ["pp", "lsb"], "tie%d" % t)
+    ts2(T.xw[:, 514:1024:4], T.q0[:], L(5), OP.is_equal, T.c512[:, 0:1], OP.mult, ["q0", "lsb", "c512"], "w22")
+    ts2(T.tie[:, NT:NT + CH], T.lrow[:], L(3), OP.subtract, L(0), OP.is_gt, ["lrow", "lsb"], "tie3")
+    for t in range(3):
+        act(T.mc[:, CH * t:CH * t + CH], T.ub[:, TRI - 128 * t:TRI - 128 * t + NT].indirect(T.lin[:]), AF.Identity,
+            T.scd[:, t:t + 1], T.dl0[:, t:t + 1], ["ubz", "tri", "ones", "lin", "scd", "dl0"], "mc%d" % t)
+    for i in range(4):
+        act(T.xw[0:CH, 96 * i + 98:96 * i + 192:4], T.mk[0:CH, :], AF.Copy, 0.0,
+            T.lsb[0:CH, 6 + i:7 + i] if i < 2 else T.nab[0:CH, i - 2:i - 1], ["mk", "lsb", "nab0", "nab1", "xz"], "xg%d" % i)
+    act(T.xw[0:CH, 483:492:8], T.lsb[0:CH, 0:4:3], AF.Copy, 0.0, 1.0, ["lsb", "xz"], "xl0")
+    act(T.thr[:, 1:48:2], T.mk[:], AF.Identity, -8.0, CH + 0.5, ["mk"], "thr3")
+    for t in range(3):
+        act(T.thr[:, 16 * t:16 * t + 16:2], T.th8[:], AF.Identity, T.gd[:, t:t + 1], 1.0, ["th8", "gd"], "thr%d" % t)
+    store("Y", [(T.li[0:1, :], T.lrow[0:1, :])], ["lrow"])
+    quant("big", HO + CH + 192, HO + CH + NT, T.hx[:, 4 * CH + 768:4 * (CH + NT)], hk("h0"), "bh0b")
+    quant("big", HO + CH, HO + CH + 192, T.hx[:, 4 * CH:4 * CH + 768], hk("h0"), "bh0a")
+    quant("xwq", 0, 256, T.xw[:], ["xz", "w20", "w21", "w22", "w23"] + hk("xg") + hk("xl", 3) + hk("xs", 3), "xwq")
 
     mk = ["bt", "bm"]
-    for c in range(3):
-        pick_s("t1", 128 * c, 128, "big", HALF, 2 * HALF, "off1", 8 * c, mk + ["off1%d" % c], "t1s%d" % c)
-        pick_c("t1", 128 * c, 128, "big", HALF, 2 * HALF, "off1", 8 * c, mk + ["off1%d" % c], "t1c%d" % c)
-        for f in (col, row):
-            f(c, "t1", "ur2", ["t1c%d" % c, "t1s%d" % c, "ur2"])
-
-    def N(what, i, bank):
-        if what == "D":
-            D(i, bank, "big", HALF, 128, mk)
-        else:
-            R(i, bank, "big", HALF, 128, "hr1", CH, mk)
-
-    score(0, 2), step(0, 2), score(2, 3), step(2, 3), shift(0)
-    cp(T.off1f[:], T.off1[:], hk("off1", 3), "off1f")
-    against(0, 1), against(1, 0)
-    sign(1, 2), shift(2)
-    against(2, 0), against(2, 1), against(0, 0)
-    sign(0, 2), shift(1), relu(1, 2), relu(0, 2)
-    quant("big", CH, CH + 192, T.hx[:, 4 * CH:4 * CH + 768], hk("h0"), "bh0a")
-    against(2, 2), against(1, 1), pack(2)
-    cp(T.lif[:], T.lin[:], ["lin"], "lif")
-    pack(1), pack(0)
-    store("Y", [(T.li[0:1, 16 * k:16 * k + 16], T.lif[0:16, k:k + 1]) for k in range(6)], ["lif"])
-    N("R", 0, 1), N("D", 0, 2), N("R", 1, 5), N("D", 1, 3)
-    N("R", 2, 7), position(2), N("R", 3, 6), position(1), position(0), N("D", 2, 1), N("D", 3, 5)
-    add(0, 2, "hx", 0, CH, "hr1", "h1")
-    add(1, 3, "hx", 0, CH, "hr1", "h1")
-    tt(T.xo[:, 0:96], T.thr[:], B(4, 0, 96), OP.is_le, ["thr", "b4"], "xo")
-
-    def rowlist(t):
-        ts(T.wx[:, 48 + t:560:4], T.pm[:], B(4, t, t + 1), OP.is_equal, ["pm", "b4", "wxq"], "wx%d" % t)
-    rowlist(0)
-    quant("xoq", 0, 128, T.xo[:], ["xoz", "xo"], "xoq")
-    mm(7, 128, "w2", 0, "xoq", 0, True, True, ["xoq", "w2"])
-    add(2, 1, "hx", 0, CH, "hr1", "h1")
-    add(3, 5, "hx", 0, CH, "hr1", "h1")
-    rowlist(1)
-    quant("big", 0, 128, T.hx[:, 0:512], hk("h0") + hk("h1") + ["bh0a"], "bh1")
-    tt(T.off2f[:], T.off1f[:], B(7, 0, 24), OP.add, ["off1f", "b7"], "off2f")
-    rowlist(2)
-    cp(T.off2[:], T.off2f[:], ["off2f"], "off2")
-    quant("wxq", 12, 140, T.wx[:, 48:560], ["wxz", "wx0", "wx1", "wx2"], "wxq")
-    mm(0, 128, "zq", 98, "wxq", 12, True, False, ["wxq", "zq"])
-    mm(0, 128, "zq", 96, "wxq", 12, False, True, ["wxq", "zq"])
+    mm(0, 128, "big", 0, "pe", CH, True, True, mk + ["ur2"])
+    mm(1, 128, "pe", CH, "big", 0, True, True, mk + ["ur2"])
+    RN, DN = (2, 3, 6, 7), (0, 5, 2, 1)
+    for i in range(4):
+        Rm(i, RN[i], "big", 0, 128, mk)
+    act(T.sm[:], B(0, 0, 1), AF.Copy, 0.0, 1.0, ["b0"], "sm")
+    act(T.dm[:], B(0, 0, 1), AF.Abs, TINY, ULP, ["b0"], "dm")
+    D(0, DN[0], "big", 0, 128, mk)
+    for t in range(4):
+        w = 128 if t < 3 else CH
+        act(T.mt[:, 128 * t:128 * t + w], T.tie[:, 128 * t:128 * t + w], AF.Identity, T.sm[:, 0:1], T.dm[:, 0:1],
+            ["tie%d" % t, "sm", "dm"], "mt%d" % t)
+    for i in range(4):
+        Ra(i, RN[i], "hr1", CH)
+    for t in range(3):
+        tt(slot(1, t, CH), B(1, 0, CH), T.mc[:, CH * t:CH * t + CH], OP.is_lt, ["b1", "mc%d" % t], "cm1%d" % t)
+    add(0, DN[0], "hx", 0, CH, "hr1", "h1")
+    pack(1)
+    mm(4, 128, "cq", 128, "zq", ZO, False, False, ["cq1", "zq"])
+    mm(4, 128, "cq", 128, "zq", ZO - 2, False, False, ["cq1", "zq"])
+    for t in range(3):
+        tt(slot(0, t), B(5, 128 * t, 128 * t + 128), T.mt[:, 128 * t:128 * t + 128], OP.is_lt, ["b5", "mt%d" % t], "cm0%d" % t)
+    tt(slot(0, 3, CH), B(1, 0, CH), T.mt[:, NT:NT + CH], OP.is_lt, ["b1", "mt3"], "cm03")
+    for i in (2, 1, 3):
+        D(i, DN[i], "big", 0, 128, mk)
+    pack(0, ["cm03"])
+    mm(4, 128, "cq", 0, "zq", ZP, False, True, zk + ["cq0"])
+    for i in range(4):
+        mm(3, 128, "xwq", 128, "xwq", 24 * i + 24, i == 0, False, ["xwq"])
+    for i in (2, 1, 3):
+        add(i, DN[i], "hx", 0, CH, "hr1", "h1")
+    tt(T.xw[:, 0:96:2], B(4, 0, 48), T.thr[:], OP.is_lt, hk("thr") + ["b4", "xwq"], "xo")
+    for t in range(4):
+        s, a = (T.gd[:, t:t + 1], 16 * t) if t < 3 else (-7.5, 1)
+        ts2(T.wx[:, 48 + t:560:4], T.pp[:], s, OP.add, B(4, a, a + 1), OP.is_equal, ["pp", "gd", "b4"], "wx%d" % t)
+    quant("xoq", 0, 128, T.xw[:, 0:512], ["xo", "xwq"], "xoq")
+    mm(3, 128, "xwq", 128, "xoq", 0, False, True, ["xoq", "xwq"])
+    quant("big", HO, HO + 128, T.hx[:, 0:512], hk("h0") + hk("h1") + ["bh0a"], "bh1")
+    cp(T.off2[:], B(3, 0, 24), ["b3"], "off2")
+    quant("wxq", 12, 140, T.wx[:, 48:560], hk("wx"), "wxq")
+    mm(6, 128, "xwq", 24, "wxq", 12, True, False, ["wxq", "xwq"])
+    mm(6, 128, "xwq", 26, "wxq", 12, False, True, ["wxq", "xwq"])
     al = ["bh0a", "bh0b", "bh1", "off2"] + mk
+    YB = (7, 0, 2)
     for c in range(3):
-        pick_s("oq", 128 * c, 128, "big", 0, 2 * HALF, "off2", 8 * c, al, "oqs%d" % c)
-        pick_c("oq", 128 * c, 128, "big", 0, 2 * HALF, "off2", 8 * c, al, "oq%d" % c)
-        mm((5, 6, 7)[c], 128, "wq", 0, "oq", 128 * c, True, True, ["wq", "oq%d" % c, "oqs%d" % c])
+        pick_s("oq", 128 * c, 128, "big", 0, HO + CH + NT, "off2", 8 * c, al, "oqs%d" % c)
+        pick_c("oq", 128 * c, 128, "big", 0, HO + CH + NT, "off2", 8 * c, al, "oq%d" % c)
+        mm(YB[c], 128, "wq", 0, "oq", 128 * c, True, True, ["wq", "oq%d" % c, "oqs%d" % c])
         if c != 1:
             a = max(128 * c - 128, 0)
             store("Y", [(T.oc[:, 4 * a:512 * c + 512], u8("oq", a, 128 * c + 128))], ["oq1", "oq2"] if c else ["oq0"])
     for c in range(2):
-        act(T.yb[:, 128 * c:128 * c + 128], B(5 + c, 0, 128), AF.Copy, 0.0, 1.0, ["b%d" % (5 + c)], "yb%d" % c)
-    cp(T.lir[:], B(0, 0, 96), ["b0"], "lir")
-    cp(T.yb[:, 256:384], B(7, 0, 128), ["b7"], "yb2")
+        act(T.yb[:, 128 * c:128 * c + 128], B(YB[c], 0, 128), AF.Copy, 0.0, 1.0, ["b%d" % YB[c]], "yb%d" % c)
+    cp(T.lir[:], B(6, 0, 96), ["b6"], "lir")
+    cp(T.yb[:, 256:384], B(YB[2], 0, 128), ["b%d" % YB[2]], "yb2")
     store("Y", [(T.osc[4 * k:4 * k + 4, :], T.oqs[32 * k:32 * k + 4, :]) for k in range(4)], hk("oqs", 3))
     for a, b in ((0, 2), (2, 3)):
         store("Y", [(T.y[:, 128 * a:128 * b], T.yb[:, 128 * a:128 * b])], ["yb%d" % c for c in range(a, b)])
-    store("S", [(T.li[1:2, :], T.lir[126:127, :])], ["lir"])
+    store("S", [(T.li[1:2, :], T.lir[96:97, :])], ["lir"])
 
+    issue()
     for q in ("V", "T", "S", "G"):
         g.wait_ge(T.sem["s" + q], cnt[q])
     g.wait_ge(T.sem["ls"], loc[0])
-    g.wait_ge(T.sem["dst"], stores[0])
+    g.wait_ge(T.sem["dst"], 16 * stores[0])

@@ -6,8 +6,8 @@ F8 = "float8_e4m3fn_x4"
 CH = 96
 NT = 384
 HO = 512
-TRI, ONE = 512, 640
-ZO, ZU, ZD, ZA, ZB, ZT, ZP, NZ = 70, 138, 206, 336, 352, 384, 392, 520
+TRI, ONE = 528, 656
+ZO, ZC, ZA, ZB, ZT, ZP, NZ = 70, 138, 224, 240, 272, 292, 420
 NA = 16
 WX = 140 + NA
 
@@ -26,20 +26,20 @@ def codes(**names):
 F, H, U = "float32", "bfloat16", "uint16"
 SCRATCH = {"ps": ("psum", [128, 4096], F)}
 SCRATCH.update({k: sb(n, d) for d, names in (
-    (H, dict(ub=896, xb=4 * NT, vb=2048, wb=512, eb=520, urb=512, q0=128, pp=128, wa=128, c75=1, zb=4 * NZ, k12=24, xw=1024,
+    (H, dict(ub=912, xb=4 * NT, vb=2048, wb=512, eb=520, urb=512, urn=512, q0=128, zb=4 * NZ, k12=24, xw=1024,
              cmp=4 * NT, sg=768, wx=4 * WX, tie=NT + CH, mk=24, hb=512, hx=4 * (CH + NT))),
     (F, dict(kc=48, jj=24, jx=24, ab=48, jbp=1, ip=1, ip1=1, ip2=1, ip3=1, p16f=1, tha=64, tj=12, t8=4, pl=NT, c96=8, c96a=8,
-             th8=8, c512=1, nab=2, sc=3, dl=3, mt=NT + CH, x0=48, sc0=3, dl0=3, mz=390, scd=3, gd=3, mc=3 * CH, lsb=8,
-             lrow=CH, thr=48, sm=1, dm=1, hrb=4 * CH, hr0=4 * NT, hr1=4 * CH, yb=NT, lir=CH)),
+             th8=8, c512=1, nab=1, sc=3, dl=3, mt=NT, x0=48, kl=48, sc0=3, dl0=3, mz=390, scd=3, gd=3, mc=3 * CH, lsb=10,
+             lrow=CH, thr=48, hrb=4 * CH, hr0=4 * NT, hr1=4 * CH, yb=NT, lir=1)),
     (U, dict(z16=8, lst1=6, lin=6, off2=24))) for k, n in names.items()})
-SCRATCH.update(codes(uq=128, ur1=128, t0=NT, vq=512, wq=128, qe=CH + 512, zq=NZ, cq=NT, wxq=WX, xwq=256,
-                     xoq=128, q1=CH, m1=128, big=HO + CH + NT, oq=NT, uin=144, pe=CH + 128))
+SCRATCH.update(codes(uq=128, ur1=128, t0=NT + 16, vq=512, wq=128, qe=CH + 512, zq=NZ, cq=NT, wxq=WX, xwq=256,
+                     xoq=128, q1=CH, m1=128, big=HO + CH + NT, oq=NT, pe=CH + 128, un=128))
 SEMAPHORES = ["sV", "sT", "sS", "sG", "du", "dx0", "dx1", "dx2", "dv0", "dv1", "dv2", "dv3", "dw", "dst",
               "au", "aq", "at", "am", "al", "aa", "go", "go2", "ls"]
 
 OP = AluOpType
 AF = ActivationFunctionType
-BIG1, BIG32 = 1.5 * 2.0 ** 23, 1.5 * 2.0 ** 28
+BIG1, BIG16, BIG32 = 1.5 * 2.0 ** 23, 1.5 * 2.0 ** 27, 1.5 * 2.0 ** 28
 ULP = 1.03125 * 2.0 ** -24
 TINY = 1e-37
 FAR = 1e29
@@ -47,19 +47,19 @@ C05 = 13421773 * 2.0 ** -28
 BANKS = ["b%d" % k for k in range(8)]
 
 ORDER = """
-ubz jj ub xb0 xb1 pp xb2 zbz jx ebz c75 ip ebz2 w23 c96 c96a urb1 uq ip1 zbz2 aba urb2 >au0 hbz q0 urb3 uinz ip2 cmk zu
-t8 ones kc zp2 t00 zo12 zd ebi jbp zp3 zo10 t01 ip3 zo11 zo13 abb p16f nab0 th8 t02 zo01 zt2 urb0 eq1 tri wa z16 eq0
-zo02 zo00 zp0 zo03 zp1 ur2 wx3 >at0 eq2 k12 >at1 xz ur1 ur1s b2 go tha b3 b1 vb0 zq nab1 vb1 tj zt1 vb2 sc b7 vb3 dl b0
-pl b6 cm21 mt2 cm20 sg1 mt1 cm22 sg0 cm10 mt0 cq2 cm12 cm11 cm02 cm00 b4 b4.2 cm01 b1.2 b2.2 cq1 b3.2 b5 cq0 sc0 xs1
-b4.3 dl0 w20 b4.4 b4.5 cm10.2 xl2 b2.3 mz1 x0 w21 wxa wx2 sg2 wx0 wxx sg5 wx1 mz2 xs2 wxq sg3 vq1 cm01.2 b0.2 vq0 zt4
-b0.3 zt5 cm20.2 cm21.2 lst1 b3.3 xl1 eq3 q1s q1 b1.3 b6.2 zt3 cm02.2 >aq0 mz0 vq3 >aq1 hr00 cm22.2 >al0 cm11.2 >aa0
-c512 vq2 zt0 hr01 cm00.2 >aa1 cq2.2 b7.2 xs0 cq0.2 b3.4 go2 zq2 hr02 wb h00 h01 h02 b4.6 b0.4 b1.4 hrb0 b6.3 b7.3 hrb1
-b2.4 hrb2 b4.7 hb0 hrb3 b0.5 hb1 b6.4 lrow hb2 hb3 b1.5 pes b1.6 b1.7 m1 b7.4 st0 hr03 pec b4.8 >am0 wq >am1 gd b2.5
-sg4 thr1 scd h03 cm12.2 lsb mc0 cq1.2 mk mc1 bh0a xl0 xg3 w22 xg0 tie0 xg1 tie1 xg2 tie2 mc2 bh0b xwq tie3 b0.6 b2.6
-b1.8 sm b7.5 dm hr10 cm12.3 mt1.2 cm11.3 b0.7 cm10.3 b4.9 mt0.2 b4.10 cm01.3 mt2.2 b2.7 cm00.3 b6.5 mt3 cq1.3 thr0 thr2
-hr12 cm02.3 thr3 cm03 b4.11 b3.5 h10 b4.12 cq0.3 b5.2 hr11 h12 hr13 b4.13 h11 b1.9 b3.6 xo b3.7 wx0.2 wx1.2 b3.8 xoq
-b3.9 h13 wx2.2 b3.10 bh1 off2 wx3.2 oq0 oqs0 oq1 oqs1 b7.6 st1 oq2 oqs2 b0.8 wxq.2 yb0 yb1 b2.8 st2 b6.6 b6.7 yb2 st3
-st7 lir st8 st9
+ub xb0 ones ubz jj jx xb1 xb2 ip ip1 q0 wx3 aba tri urb2 nab0 zbz zc1 zc2 zo03 jbp zo12 ip2 urb0 zc0 urb3 urb1 zo11
+zo10 uq >au0 t00 z16 t01 zbz2 t02 b1 ur2 ebi eq0 eq3 >at0 >at1 go vb0 kc cmk eq1 zp0 tj zp3 vb1 vb2 vb3 zt4 zo01 ip3
+zo00 abb urn un0 zt1 p16f wa zo02 zt7 zt3 zo13 w21 ur1s w20 ur1 zq eq2 b2 b3 sc b0 cm01 b7 cm21 dl zt6 cm20 mt2 cm22
+mt1 b6 sg1 sg0 cm10 cm11 cq2 mt0 cm00 zt5 cm12 cq1 cm02 t8 zt2 b2.2 b5 b3.2 b1.2 sc0 dl0 mz1 mz2 sg2 sg3 cq0 b4 b4.2
+b4.3 vq0 cm01.2 mz0 kl tha wxa zp1 xz pp zp2 x0 wx2 wx0 wx1 wxx cm20.2 wxq >aa0 >aa1 xs1 zt0 zq2 vq1 b3.3 b2.3 b0.2
+b0.3 lst1 b1.3 cm22.2 b6.2 q1 vq2 b7.2 xl2 cm02.2 hr00 b3.4 h60 vq3 >aq0 q1s >aq1 b4.4 >al0 go2 wb xs0 c96 k12 sg4 sg5
+hr01 xl1 h50 h70 cm00.2 h71 cm11.2 cm10.2 h61 h51 cm21.2 cq2.2 cm12.2 hr02 cq1.2 pec hrb0 b6.3 hrb2 b1.4 b0.4 hrb1 hb0
+b7.3 b2.4 hb1 b4.5 hb2 b0.5 hrb3 hb3 pes h62 pl lrow st0 b1.5 b1.6 b1.7 gd b2.5 b2.6 lsb ls9 b6.4 hr03 m1 cq0.2 b4.6
+scd h72 c96a th8 c512 >am0 w22 >am1 mk tie1 tie3 xg0 tie0 h52 b7.4 h73 h53 tie2 h63 wa.2 wq bh6 bh5 b4.7 b5.2 b4.8 b2.7
+b3.5 thr1 mc1 xl0 xs2 xg2 mc2 mc0 b1.8 cm11.3 cm12.3 thr2 thr3 cm10.3 b5.3 cm00.3 xg1 b6.5 b3.6 cm02.3 b2.8 b0.6 b0.7
+cm01.3 cm03 cq1.3 bh7 cq0.3 thr0 b7.5 xwq hr10 b6.6 b1.9 h10 b4.9 hr11 b0.8 h11 b7.6 b4.10 xo wx2.2 hr12 b5.4 h12 hr13
+xoq wx3.2 b3.7 b2.9 h13 wx1.2 wx0.2 bh1 b3.8 off2 wxq.2 b6.7 oq0 st1 oqs0 oqs1 oqs2 b7.7 yb0 oq1 b0.9 oq2 st2 lir st9
+yb1 st3 b2.10 yb2 st7 st8
 """
 
 
@@ -201,9 +201,6 @@ def rank_program(g, core, T, topo):
     def ones(w):
         return T.ub[:, ONE:ONE + w]
 
-    def zero(out, w, key):
-        S(lambda e: e.activation(out, zeros(w), AF.Copy), ["ubz"], key)
-
     def quant(out, a, b, src, reads, key):
         V(lambda e: e.quantize_mx(T[out][:, a:b], T[out + "s"][:, a:b], src), reads, key)
 
@@ -225,34 +222,33 @@ def rank_program(g, core, T, topo):
     def hk(key, k=4):
         return [key + str(i) for i in range(k)]
 
+    pp = T.hb[:, 4 * CH:512]
+    wa = T.xw[:, 515:1024:4]
+
     dma("Y", [(T.ub[:, 0:8], T.u[:, 0:8])], "du", 16, [], ["ub"])
     for c in range(3):
         dma("Y", [(T.xb[:, 512 * c:512 * c + 512], T.x[:, 512 * c:512 * c + 512])], "dx%d" % c, 16, [], ["xb%d" % c])
 
-    memset(T.ub[:, 8:512], 0.0, "ubz")
+    memset(T.ub[:, 8:TRI], 0.0, "ubz")
     memset(ones(256), 1.0, "ones")
     iota(T.jj[:], [[0, 6], [128, 4]], "jj", 1)
     iota(T.ip[:], [[0, 1]], "ip", 2)
-    asel(T.c75[:], zeros(1), [[1, 1]], OP.not_equal, -7.5, 0, 1, ["ubz"], "c75")
     iota(T.q0[:], [[0, 8], [1, 16]], "q0")
     memset(T.z16[:], 0, "z16")
     memset(T.zb[:, 0:4 * ZA], 0.0, "zbz")
     quant("uq", 0, 128, T.ub[:, 0:512], ["ub", "ubz"], "uq")
-    quant("uin", 0, 128, T.zb[:, 0:512], ["zbz"], "uinz")
     rid, pid, _ = topo.addr(prv)
     e0 = half(prv, 0)
     op("G", lambda e: e.remote_dma_fused(
         [RemoteDMATransfer(dst_ids=[DstId(rid=rid, pnc=pid)], dma_engine_mask=bits(e0[:4]), remote_sem=T.sem["au"],
-                           src=u8("uq", 0, 2), dst=u8("uin", 128, 130)),
+                           src=u8("uq", 0, 2), dst=u8("t0", NT, NT + 2)),
          RemoteDMATransfer(dst_ids=[DstId(rid=rid, pnc=pid)], dma_engine_mask=bits(e0[4:]), remote_sem=T.sem["au"],
-                           src=T.uqs[:, 0:8], dst=T.uins[:, 128:136])], local_sem=T.sem["ls"]), ["uq"], [">au0"], "")
+                           src=T.uqs[:, 0:8], dst=T.t0s[:, NT:NT + 8])], local_sem=T.sem["ls"]), ["uq"], [">au0"], "")
     loc[0] += len(e0)
-    zero(T.eb[:, 0:504], 504, "ebz")
-    zero(T.eb[:, 504:520], 16, "ebz2")
-    asel(T.eb[:, 4:516:4], ones(128), [[-1, 128]], OP.is_equal, 0.0, 0, 1, ["ones", "ebz", "ebz2"], "ebi")
+    asel(T.eb[:], zeros(520), [[-1, 130], [1000, 4]], OP.not_equal, 1.0, 1, 1, ["ubz"], "ebi")
     asel(T.ub[:, TRI:ONE], ones(128), [[1, 128]], OP.is_gt, 0.0, 0, -1, ["ones"], "tri")
     iota(T.kc[:], [[0, 2], [16, 6], [0, 4]], "kc")
-    iota(T.tha[:], [[0, 8], [1000, 2], [0, 4]], "tha", 0, CH)
+    iota(T.tha[:], [[0, 8], [1000, 2], [0, 4]], "tha", 0, CH - 8)
     act(T.jx[:], T.jj[:], AF.Identity, BIG32, 1.0, ["jj"], "jx")
     act(T.ip1[:], T.ip[:], AF.Identity, -15.0, 1.0, ["ip"], "ip1")
     act(T.ab[:, 0:24], T.jx[:], AF.Identity, -BIG32, 1.0, ["jx"], "aba")
@@ -260,28 +256,24 @@ def rank_program(g, core, T, topo):
     act(T.jbp[:], T.ab[:, 0:1], AF.Identity, T.jj[:, 0:1], -1.0, ["aba", "jj"], "jbp")
     act(T.ip3[:], T.ip2[:], AF.Identity, -BIG1, 1.0, ["ip2"], "ip3")
     act(T.ab[:, 24:48], zeros(24), AF.Identity, T.jbp[:, 0:1], 1.0, ["ubz", "jbp"], "abb")
-    act(T.cmp[:, 3:4 * NT:4], zeros(NT), AF.Identity, T.c75[:, 0:1], 1.0, ["ubz", "c75"], ["cmk", "cm03"])
+    asel(T.cmp[:, 3:4 * NT:4], zeros(NT), [[0, NT]], OP.not_equal, -7.5, 0, 1, ["ubz"], ["cmk", "cm03"])
     act(T.p16f[:], T.ip3[:], AF.Identity, T.jj[:, 0:1], -16.0, ["ip3", "jj"], "p16f")
-    zero(T.wx[:, 51:560:4], 128, "wx3")
+    act(T.wx[:, 51:560:4], zeros(128), AF.Copy, 0.0, 1.0, ["ubz"], "wx3")
     for t in range(4):
         for a in range(2):
             k = 17 if t < 3 else 16
             b = (8, 4 * ZO + 4)[a]
-            act(T.zb[:, b + t:b + 16 * k:16], ones(k), AF.Copy, 0.0, 1.0, ["ones", "zbz", "uinz"], "zo%d%d" % (a, t))
-    memset(T.zb[0:1, 4 * ZU + 3:4 * ZU + 256:4], -2.0 ** 25, "zu", ["zbz", "uinz"])
-    memset(T.zb[0:1, 4 * ZD + 3:4 * ZD + 256:4], 2.0 ** 25, "zd", ["zbz", "uinz"])
+            act(T.zb[:, b + t:b + 16 * k:16], ones(k), AF.Copy, 0.0, 1.0, ["ones", "zbz"], "zo%d%d" % (a, t))
+    for t in range(3):
+        act(T.zb[:, 4 * ZC + 4 + t:4 * ZC + 192:8], ones(24), AF.Copy, 0.0, 1.0, ["ones", "zbz"], "zc%d" % t)
     for t in range(4):
         act(T.urb[:, t:512:4], zeros(128), AF.Identity, T.ub[:, t:t + 1], 1.0, ["ub", "ubz"], "urb%d" % t)
-    zero(T.hb[:, 4 * CH:512], 128, "hbz")
-    act(T.wa[:], T.q0[:], AF.Abs, T.p16f[:, 0:1], -1.0, ["q0", "p16f"], "wa")
-    zero(T.xw[:, 515:1024:4], 128, "w23")
+    act(wa, T.q0[:], AF.Abs, T.p16f[:, 0:1], -1.0, ["q0", "p16f"], "wa")
 
-    def EQ(b):
-        quant("qe", CH + 128 * b, CH + 128 * b + 128, T.eb[:, 4 - b:516 - b], ["ebz", "ebz2", "ebi"], "eq%d" % b)
     for c in range(3):
         quant("t0", 128 * c, 128 * c + 128, T.xb[:, 512 * c:512 * c + 512], ["xb%d" % c], "t0%d" % c)
     for b in range(4):
-        EQ(b)
+        quant("qe", CH + 128 * b, CH + 128 * b + 128, T.eb[:, 4 - b:516 - b], ["ebi"], "eq%d" % b)
     t0 = hk("t0", 3)
     send(nx2, u8("big", CH, CH + NT), u8("t0", 0, NT), "at", topo.engines(core, nx2), t0)
     send(nx2, T.bigs[:, CH:CH + NT], T.t0s[:, 0:NT], "at", topo.engines(core, nx2), t0)
@@ -291,7 +283,7 @@ def rank_program(g, core, T, topo):
     iota(T.tj[:], [[-128, 3], [128, 4]], "tj")
     iota(T.t8[:], [[8, 4]], "t8", 0, -12)
     iota(T.xw[:, 0:512], [[0, 512]], "xz")
-    iota(T.pp[:], [[1, 128]], "pp")
+    iota(pp, [[1, 128]], "pp")
     iota(T.xw[0:32, 1:96:4], [[16, 24]], "xs0", 0, -192, ["xz"])
     memset(T.xw[32:64, 1:96:4], 192.0 + CH, "xs1", ["xz"])
     iota(T.c96[:], [[0, 8]], "c96", 0, CH)
@@ -302,10 +294,12 @@ def rank_program(g, core, T, topo):
     iota(T.pl[:], [[1, NT]], "pl")
     memset(T.zb[:, 4 * ZB:4 * NZ], 0.0, "zbz2")
     for t in range(3):
-        memset(T.zb[0:CH, 4 * ZP + 65 * t:4 * ZP + 64 * t + 64:8], 1.0, "zp%d" % t, ["zbz2"])
-    memset(T.zb[0:CH, 4 * ZP + 7:4 * ZP + 192:8], 1.0, "zp3", ["zbz2"])
-    quant("zq", 0, ZA, T.zb[:, 0:4 * ZA], ["zbz", "zu", "zd"] + hk("zo0") + hk("zo1"), "zq")
+        iota(T.zb[0:CH, 4 * ZP + 65 * t:4 * ZP + 64 * t + 64:8], [[0, 8]], "zp%d" % t, 0, 1, ["zbz2"])
+    iota(T.zb[0:CH, 4 * ZP + 7:4 * ZP + 192:8], [[0, 24]], "zp3", 0, 1, ["zbz2"])
+    quant("zq", 0, ZA, T.zb[:, 0:4 * ZA], ["zbz"] + hk("zo0") + hk("zo1") + hk("zc", 3), "zq")
     quant("pe", CH, CH + 128, T.urb[:], hk("urb"), "ur2")
+    act(T.urn[:], T.urb[:], AF.Copy, 0.0, -1.0, hk("urb"), "urn")
+    quant("un", 0, 128, T.urn[:], ["urn"], "un0")
 
     ROW = (0, 6, 7)
     SC = 126
@@ -337,7 +331,7 @@ def rank_program(g, core, T, topo):
         quant("cq", 128 * c, 128 * c + 128, T.cmp[:, 512 * c:512 * c + 512], hk("cm%d" % c, 3) + ["cmk"] + list(more), "cq%d" % c)
 
     def position(c):
-        mm(4, 128, "cq", 128 * c, "zq", (2, ZO, 0)[c], False, False, ["cq%d" % c, "zq"])
+        mm(4, 128, "cq", 128 * c, "zq", (2, ZO, 0)[c], c == 2, c == 0, ["cq%d" % c, "zq"])
 
     def Rm(i, bank, q, q0, w, keys):
         mm(bank, w, "vq", 128 * i, q, q0, True, True, keys + ["vq%d" % i])
@@ -359,25 +353,22 @@ def rank_program(g, core, T, topo):
         Ra(i, bank, "hr0", NT)
 
     def A0(i, bank):
-        add(i, bank, "hx", CH, NT, "hr0", "h0")
+        for c in range(3):
+            a = 4 * (CH + 128 * c)
+            tt(T.hx[:, a + i:a + 512:4], T.hr0[:, NT * i + 128 * c:NT * i + 128 * c + 128], B(bank, 128 * c, 128 * c + 128),
+               OP.add, ["hr0%d" % i, "b%d" % bank], "h%d%d" % (c + 5, i))
 
-    def VQ(i):
-        quant("vq", 128 * i, 128 * i + 128, T.vb[:, 512 * i:512 * i + 512], ["vb%d" % i], "vq%d" % i)
-
-    uk = ["uin", "uinz"]
     for c in range(3):
-        mm(1 + c, 128, "t0", 128 * c, "uin", 2, True, True, ["t0%d" % c] + uk)
-    pick_s("ur1", 0, 128, "uin", 128, 130, "z16", 0, uk + ["z16"], "ur1s")
-    pick_c("ur1", 0, 128, "uin", 128, 130, "z16", 0, uk + ["z16"], "ur1")
+        mm(1 + c, 128, "t0", 128 * c, "t0", NT - SC, True, True, ["t0%d" % c, "t02", "uin"])
+    pick_s("ur1", 0, 128, "t0", NT, NT + 2, "z16", 0, ["uin", "z16"], "ur1s")
+    pick_c("ur1", 0, 128, "t0", NT, NT + 2, "z16", 0, ["uin", "z16"], "ur1")
     for c in (2, 0, 1):
         mm(ROW[c], 128, "ur1", 0, "t0", 128 * c, True, True, ["t0%d" % c, "ur1", "ur1s"])
     score("sc", "dl", SC), shift(2), sign(0, 2), sign(1, 2), shift(1), shift(0), relu(1, 2, 1), relu(0, 2, 0)
     for c, t in ((2, 0), (2, 1), (2, 2), (0, 1), (1, 0), (1, 1)):
         against(c, t)
     pack(2), against(0, 0), pack(1), pack(0)
-    mm(4, 128, "cq", 256, "zq", ZU, True, False, ["cq2", "zq"])
     position(2), position(1), position(0)
-    mm(4, 128, "cq", 0, "zq", ZD, False, True, ["cq0", "zq"])
     for c in range(3):
         mm(1 + c, 128, "big", CH + 128 * c, "pe", CH, True, True, ["bt", "ur2"])
     mm(5, NT, "pe", CH, "big", CH, True, True, ["bt", "ur2"])
@@ -387,40 +378,42 @@ def rank_program(g, core, T, topo):
     act(T.zb[:, zt + 16:zt + 20], T.t8[:], AF.Identity, T.ip3[:, 0:1], 1.0, ["t8", "ip3", "zbz2"], "zt2")
     act(T.zb[:, zt + 20:zt + 24], zeros(4), AF.Identity, T.p16f[:, 0:1], 1.0, ["ubz", "p16f", "zbz2"], "zt3")
     act(T.zb[:, zt + 24:zt + 28], T.ab[:, 0:4], AF.Copy, 0.0, -1.0 / HO, ["aba", "zbz2"], "zt4")
-    act(T.zb[:, zt + 28:zt + 32], T.ab[:, 24:28], AF.Copy, 0.0, -1.0 / HO, ["abb", "zbz2"], "zt5")
-    act(T.xw[:, 512:1024:4], T.wa[:], AF.Relu, float(HO), -float(HO), ["wa"], "w20")
-    act(T.xw[:, 513:1024:4], T.wa[:], AF.Relu, 0.5, -0.5, ["wa"], "w21")
-    act(T.nab[:, 0:1], T.ab[:, 0:1], AF.Identity, -CH / HO, 1.0 / HO, ["aba"], "nab0")
-    act(T.nab[:, 1:2], T.jbp[:], AF.Copy, 0.0, 1.0 / HO, ["jbp"], "nab1")
-    act(T.xw[:, 480:483], T.ab[:, 0:3], AF.Copy, 0.0, 1.0, ["aba", "xz"], "xl1")
-    act(T.xw[:, 488:491], T.ab[:, 24:27], AF.Copy, 0.0, 1.0, ["abb", "xz"], "xl2")
+    act(T.zb[:, zt + 28:zt + 32], T.ab[:, 24:28], AF.Copy, 0.0, -1.0, ["abb", "zbz2"], "zt5")
+    act(T.zb[:, zt + 32:zt + 36], T.ab[:, 0:4], AF.Copy, 0.0, 1.0, ["aba", "zbz2"], "zt6")
+    act(T.zb[:, zt + 40:zt + 52], T.ab[:, 24:36], AF.Copy, 0.0, 1.0, ["abb", "zbz2"], "zt7")
+    act(T.xw[:, 512:1024:4], wa, AF.Relu, float(HO), -float(HO), ["wa"], "w20")
+    act(T.xw[:, 513:1024:4], wa, AF.Relu, 0.5, -0.5, ["wa"], "w21")
+    act(T.nab[:], T.ab[:, 0:1], AF.Identity, -CH / HO, 1.0 / HO, ["aba"], "nab0")
+    act(T.xw[:, 488:491], T.ab[:, 0:3], AF.Copy, 0.0, 1.0, ["aba", "xz"], "xl1")
+    act(T.xw[:, 480:483], T.ab[:, 24:27], AF.Copy, 0.0, 1.0, ["abb", "xz"], "xl2")
     act(T.xw[64:96, 1:96:4], T.ub[64:96, 8:32], AF.Identity, T.p16f[64:96, 0:1], 1.0, ["ubz", "p16f", "xz"], "xs2")
     score("sc0", "dl0", 0)
     for c in range(3):
         act(T.mz[:, 130 * c:130 * c + 129], T.ub[:, TRI:ONE + 1], AF.Identity, T.sc0[:, c:c + 1], T.dl0[:, c:c + 1],
             ["tri", "ones", "sc0", "dl0"], "mz%d" % c)
     tt(T.wx[:, 560:560 + 4 * NA], T.tha[:], B(4, 0, 4 * NA), OP.is_le, ["tha", "b4"], "wxa")
-    tt(T.x0[:], B(4, 0, 48), T.kc[:], OP.is_equal, ["b4", "kc"], "x0")
+    ts2(T.kl[:], B(4, 0, 48), BIG16, OP.add, BIG16, OP.subtract, ["b4"], "kl")
+    tt(T.x0[:], T.kl[:], T.kc[:], OP.is_equal, ["kl", "kc"], "x0")
     for t in range(3):
-        ts2(T.wx[:, 48 + t:560:4], T.q0[:], B(4, t, t + 1), OP.add, B(4, 64 + t, 65 + t), OP.is_equal, ["q0", "b4"], "wx%d" % t)
+        ts2(T.wx[:, 48 + t:560:4], T.q0[:], T.kl[:, t:t + 1], OP.add, B(4, 64 + t, 65 + t), OP.is_equal, ["q0", "b4", "kl"], "wx%d" % t)
     tt(T.wx[:, 0:48], T.x0[:], T.ab[:], OP.mult, ["x0", "aba", "abb"], "wxx")
     quant("wxq", 0, WX, T.wx[:], hk("wx") + ["wxx", "wxa"], ["wxq", "wxqa"])
     mm(0, 128, "wxq", 12, "wxq", 0, True, False, ["wxq"])
     mm(0, 128, "wxq", 12, "wxq", 6, False, True, ["wxq"])
     D0(0, 1), D0(1, 2)
-    quant("zq", ZB, NZ, T.zb[:, 4 * ZB:4 * NZ], ["zbz2"] + hk("zp") + hk("zt", 6), "zq2")
+    quant("zq", ZB, NZ, T.zb[:, 4 * ZB:4 * NZ], ["zbz2"] + hk("zp") + hk("zt", 8), "zq2")
     cp(T.lst1[:], B(0, 0, 6), ["b0"], "lst1")
+    send(nx2, u8("zq", ZA, ZA + NA), u8("wxq", 140, WX), "aa", half(nx2, 1), ["wxqa"])
+    send(nx2, T.zqs[:, ZA:ZA + NA], T.wxqs[:, 140:WX], "aa", half(nx2, 0), ["wxqa"])
     pick_s("q1", 0, CH, "t0", 0, NT, "lst1", 0, t0 + ["lst1"], "q1s")
     pick_c("q1", 0, CH, "t0", 0, NT, "lst1", 0, t0 + ["lst1"], "q1")
     send(nxt, u8("qe", 0, CH), u8("q1", 0, CH), "aq", topo.engines(core, nxt), ["q1"])
     send(nxt, T.qes[:, 0:CH], T.q1s[:, 0:CH], "aq", topo.engines(core, nxt), ["q1s"])
-    send(nx2, T.lin[:], T.lst1[:], "al", half(nx2, 0), ["lst1"])
-    send(nx2, u8("zq", ZA, ZA + NA), u8("wxq", 140, WX), "aa", half(nx2, 1), ["wxqa"])
-    send(nx2, T.zqs[:, ZA:ZA + NA], T.wxqs[:, 140:WX], "aa", half(nx2, 0), ["wxqa"])
+    send(nx2, T.lin[:], T.lst1[:], "al", half(nx2, 1), ["lst1"])
     op("G", lambda e: e.sem_inc(T.sem["go2"], 1), [">aq0", ">aq1"], ["go2"], "go2", 1)
-    dma("Y", [(T.wb[:], T.w[:])], "dw", 16, ["go2"], ["wb"])
+    dma("Y", [(T.wb[:], T.w[:])], "dw", 16, ["go2", "qin"], ["wb"])
     for i in range(4):
-        VQ(i)
+        quant("vq", 128 * i, 128 * i + 128, T.vb[:, 512 * i:512 * i + 512], ["vb%d" % i], "vq%d" % i)
 
     for c in (1, 2):
         ts(slot(c, 0), B(5, 128 * c, 128 * c + 128), T.sc0[:, 0:1], OP.is_le, ["b5", "sc0"], "cm%d0" % c)
@@ -443,7 +436,7 @@ def rank_program(g, core, T, topo):
         D(i, DB[i], "qe", 0, 128, ["qin", "eq0"])
     for i in range(4):
         add(i, DB[i], "hb", 0, CH, "hrb", "hb")
-    quant("m1", 0, 128, T.hb[:], ["hbz"] + hk("hb"), "m1")
+    quant("m1", 0, 128, T.hb[:], ["pp"] + hk("hb"), "m1")
     send(nxt, u8("big", 0, CH), u8("m1", 0, CH), "am", topo.engines(core, nxt), ["m1"])
     send(nxt, T.bigs[:, 0:CH], T.m1s[:, 0:CH], "am", topo.engines(core, nxt), ["m1"])
 
@@ -451,14 +444,15 @@ def rank_program(g, core, T, topo):
     ek = hk("eq", 3) + ["lin"]
     pick_s("pe", 0, CH, "qe", CH, CH + NT, "lin", 0, ek, "pes")
     pick_c("pe", 0, CH, "qe", CH, CH + NT, "lin", 0, ek, "pec")
-    S(lambda e: e.activation(T.lrow[:], T.pl[:].indirect(T.lin[:]), AF.Copy), ["pl", "lin"], "lrow")
+    act(T.lrow[:], T.pl[:].indirect(T.lin[:]), AF.Copy, 0.0, 1.0, ["pl", "lin"], "lrow")
     R0(3, 6), D0(3, 7)
     for t in range(3):
         mm(1, 128, "qe", CH + 128 * t, "zq", ZA - 16 * t, t == 0, t == 2, zk + ["eq%d" % t])
-    mm(2, 128, "pe", 0, "zq", ZA, True, True, zk + ["pes", "pec", "ur2"])
+    mm(2, 128, "pe", 0, "zq", ZA, True, False, zk + ["pes", "pec", "ur2"])
+    mm(2, 128, "pe", 0, "zq", ZA + 10, False, True, zk + ["pes", "pec", "ur2"])
     for c in range(3):
         mm(4, 128, "cq", 128 * c, "zq", ZA - 16 * c, c == 0, False, zk + ["cq%d" % c])
-    act(T.lsb[:], B(2, ZT - ZA, ZT - ZA + 8), AF.Copy, 0.0, 1.0, ["b2"], "lsb")
+    act(T.lsb[:, 0:9], B(2, ZT - ZA, ZT - ZA + 9), AF.Copy, 0.0, 1.0, ["b2"], "lsb")
     act(T.gd[:], B(1, 0, 48, 16), AF.Identity, -FAR, FAR, ["b1"], "gd")
     quant("wq", 0, 128, T.wb[:], ["wb"], "wq")
     A0(3, 7)
@@ -468,68 +462,64 @@ def rank_program(g, core, T, topo):
     tt(T.scd[:], T.sc0[:], T.gd[:], OP.add, ["sc0", "gd"], "scd")
     ts(T.mk[:], T.k12[:], L(4), OP.is_equal, ["k12", "lsb"], "mk")
     for t in range(3):
-        ts2(T.tie[:, 128 * t:128 * t + 128], T.pp[:], L(3), OP.subtract, L(t), OP.is_gt, ["pp", "lsb"], "tie%d" % t)
+        ts2(T.tie[:, 128 * t:128 * t + 128], pp, L(t), OP.is_gt, TINY, OP.mult, ["pp", "lsb"], "tie%d" % t)
     ts2(T.xw[:, 514:1024:4], T.q0[:], L(5), OP.is_equal, T.c512[:, 0:1], OP.mult, ["q0", "lsb", "c512"], "w22")
-    ts2(T.tie[:, NT:NT + CH], T.lrow[:], L(3), OP.subtract, L(0), OP.is_gt, ["lrow", "lsb"], "tie3")
+    ts(wa, T.q0[:], L(5), OP.is_equal, ["q0", "lsb"], "wa")
+    act(T.lsb[:, 9:10], L(6), AF.Identity, T.nab[:, 0:1], 1.0, ["lsb", "nab0"], "ls9")
+    ts2(T.tie[:, NT:NT + CH], T.lrow[:], L(0), OP.is_gt, TINY, OP.mult, ["lrow", "lsb"], "tie3")
     for t in range(3):
         act(T.mc[:, CH * t:CH * t + CH], T.ub[:, TRI - 128 * t:TRI - 128 * t + NT].indirect(T.lin[:]), AF.Identity,
             T.scd[:, t:t + 1], T.dl0[:, t:t + 1], ["ubz", "tri", "ones", "lin", "scd", "dl0"], "mc%d" % t)
-    for i in range(4):
-        act(T.xw[0:CH, 96 * i + 98:96 * i + 192:4], T.mk[0:CH, :], AF.Copy, 0.0,
-            T.lsb[0:CH, 6 + i:7 + i] if i < 2 else T.nab[0:CH, i - 2:i - 1], ["mk", "lsb", "nab0", "nab1", "xz"], "xg%d" % i)
-    act(T.xw[0:CH, 483:492:8], T.lsb[0:CH, 0:4:3], AF.Copy, 0.0, 1.0, ["lsb", "xz"], "xl0")
-    act(T.thr[:, 1:48:2], T.mk[:], AF.Identity, -8.0, CH + 0.5, ["mk"], "thr3")
+    for i, (at, c) in enumerate(((98, T.lsb[0:CH, 9:10]), (99, T.lsb[0:CH, 7:8]), (3, T.jbp[0:CH, 0:1]))):
+        act(T.xw[0:CH, at:at + 96:4], T.mk[0:CH, :], AF.Copy, 0.0, c, ["mk", "lsb", "ls9", "jbp", "xz"], "xg%d" % i)
+    act(T.xw[0:CH, 483:492:8], T.lsb[0:CH, 3:9:5], AF.Copy, 0.0, 1.0, ["lsb", "xz"], "xl0")
+    act(T.thr[:, 1:48:2], T.mk[:], AF.Copy, 0.0, float(CH), ["mk"], "thr3")
     for t in range(3):
         act(T.thr[:, 16 * t:16 * t + 16:2], T.th8[:], AF.Identity, T.gd[:, t:t + 1], 1.0, ["th8", "gd"], "thr%d" % t)
+    AB = (5, 2, 3)
+    for t in range(3):
+        mm(AB[t], 128, "pe", CH, "big", CH + 128 * t, True, False, ["bt", "ur2"])
     store("Y", [(T.li[0:1, :], T.lrow[0:1, :])], ["lrow"])
-    quant("big", HO + CH + 192, HO + CH + NT, T.hx[:, 4 * CH + 768:4 * (CH + NT)], hk("h0"), "bh0b")
-    quant("big", HO + CH, HO + CH + 192, T.hx[:, 4 * CH:4 * CH + 768], hk("h0"), "bh0a")
-    quant("xwq", 0, 256, T.xw[:], ["xz", "w20", "w21", "w22", "w23"] + hk("xg") + hk("xl", 3) + hk("xs", 3), "xwq")
+    for c in range(3):
+        a = CH + 128 * c
+        quant("big", HO + a, HO + a + 128, T.hx[:, 4 * a:4 * a + 512], hk("h%d" % (c + 5)), "bh%d" % (c + 5))
+    quant("xwq", 0, 256, T.xw[:], ["xz", "w20", "w21", "w22", "wa"] + hk("xg", 3) + hk("xl", 3) + hk("xs", 3), "xwq")
 
     mk = ["bt", "bm"]
-    mm(0, 128, "big", 0, "pe", CH, True, True, mk + ["ur2"])
     mm(1, 128, "pe", CH, "big", 0, True, True, mk + ["ur2"])
-    RN, DN = (2, 3, 6, 7), (0, 5, 2, 1)
+    for t in range(3):
+        mm(AB[t], 128, "big", 0, "un", 0, False, True, mk + ["un0"])
+    mm(0, 128, "pe", CH, "big", 0, True, False, mk + ["ur2"])
+    mm(0, 128, "big", 0, "un", 0, False, True, mk + ["un0"])
+    RN, DN = (6, 7, 6, 7), (1, 0, 5, 2)
     for i in range(4):
         Rm(i, RN[i], "big", 0, 128, mk)
-    act(T.sm[:], B(0, 0, 1), AF.Copy, 0.0, 1.0, ["b0"], "sm")
-    act(T.dm[:], B(0, 0, 1), AF.Abs, TINY, ULP, ["b0"], "dm")
-    D(0, DN[0], "big", 0, 128, mk)
-    for t in range(4):
-        w = 128 if t < 3 else CH
-        act(T.mt[:, 128 * t:128 * t + w], T.tie[:, 128 * t:128 * t + w], AF.Identity, T.sm[:, 0:1], T.dm[:, 0:1],
-            ["tie%d" % t, "sm", "dm"], "mt%d" % t)
-    for i in range(4):
         Ra(i, RN[i], "hr1", CH)
     for t in range(3):
         tt(slot(1, t, CH), B(1, 0, CH), T.mc[:, CH * t:CH * t + CH], OP.is_lt, ["b1", "mc%d" % t], "cm1%d" % t)
-    add(0, DN[0], "hx", 0, CH, "hr1", "h1")
     pack(1)
-    mm(4, 128, "cq", 128, "zq", ZO, False, False, ["cq1", "zq"])
-    mm(4, 128, "cq", 128, "zq", ZO - 2, False, False, ["cq1", "zq"])
+    mm(4, 128, "cq", 128, "zq", ZC, False, False, zk + ["cq1"])
     for t in range(3):
-        tt(slot(0, t), B(5, 128 * t, 128 * t + 128), T.mt[:, 128 * t:128 * t + 128], OP.is_lt, ["b5", "mt%d" % t], "cm0%d" % t)
-    tt(slot(0, 3, CH), B(1, 0, CH), T.mt[:, NT:NT + CH], OP.is_lt, ["b1", "mt3"], "cm03")
-    for i in (2, 1, 3):
+        tt(slot(0, t), B(AB[t], 0, 128), T.tie[:, 128 * t:128 * t + 128], OP.is_lt, ["b%d" % AB[t], "tie%d" % t], "cm0%d" % t)
+    tt(slot(0, 3, CH), B(0, 0, CH), T.tie[:, NT:NT + CH], OP.is_lt, ["b0", "tie3"], "cm03")
+    for i in range(4):
         D(i, DN[i], "big", 0, 128, mk)
     pack(0, ["cm03"])
     mm(4, 128, "cq", 0, "zq", ZP, False, True, zk + ["cq0"])
+    mm(3, 128, "xwq", 128, "xwq", 24, True, False, ["xwq"])
     for i in range(4):
-        mm(3, 128, "xwq", 128, "xwq", 24 * i + 24, i == 0, False, ["xwq"])
-    for i in (2, 1, 3):
         add(i, DN[i], "hx", 0, CH, "hr1", "h1")
     tt(T.xw[:, 0:96:2], B(4, 0, 48), T.thr[:], OP.is_lt, hk("thr") + ["b4", "xwq"], "xo")
     for t in range(4):
-        s, a = (T.gd[:, t:t + 1], 16 * t) if t < 3 else (-7.5, 1)
-        ts2(T.wx[:, 48 + t:560:4], T.pp[:], s, OP.add, B(4, a, a + 1), OP.is_equal, ["pp", "gd", "b4"], "wx%d" % t)
+        s, a = (T.gd[:, t:t + 1], 16 * t) if t < 3 else (0.0, 1)
+        ts2(T.wx[:, 48 + t:560:4], pp, s, OP.add, B(4, a, a + 1), OP.is_equal, ["pp", "gd", "b4"], "wx%d" % t)
     quant("xoq", 0, 128, T.xw[:, 0:512], ["xo", "xwq"], "xoq")
     mm(3, 128, "xwq", 128, "xoq", 0, False, True, ["xoq", "xwq"])
-    quant("big", HO, HO + 128, T.hx[:, 0:512], hk("h0") + hk("h1") + ["bh0a"], "bh1")
+    quant("big", HO, HO + 128, T.hx[:, 0:512], hk("h5") + hk("h1") + ["bh5"], "bh1")
     cp(T.off2[:], B(3, 0, 24), ["b3"], "off2")
     quant("wxq", 12, 140, T.wx[:, 48:560], hk("wx"), "wxq")
-    mm(6, 128, "xwq", 24, "wxq", 12, True, False, ["wxq", "xwq"])
-    mm(6, 128, "xwq", 26, "wxq", 12, False, True, ["wxq", "xwq"])
-    al = ["bh0a", "bh0b", "bh1", "off2"] + mk
+    mm(6, 128, "wxq", 12, "xwq", 0, True, True, ["wxq", "xwq"])
+    al = ["bh5", "bh6", "bh7", "bh1", "off2"] + mk
     YB = (7, 0, 2)
     for c in range(3):
         pick_s("oq", 128 * c, 128, "big", 0, HO + CH + NT, "off2", 8 * c, al, "oqs%d" % c)
@@ -540,12 +530,12 @@ def rank_program(g, core, T, topo):
             store("Y", [(T.oc[:, 4 * a:512 * c + 512], u8("oq", a, 128 * c + 128))], ["oq1", "oq2"] if c else ["oq0"])
     for c in range(2):
         act(T.yb[:, 128 * c:128 * c + 128], B(YB[c], 0, 128), AF.Copy, 0.0, 1.0, ["b%d" % YB[c]], "yb%d" % c)
-    cp(T.lir[:], B(6, 0, 96), ["b6"], "lir")
+    ts(T.lir[:], B(6, 120, 121), B(6, 122, 123), OP.add, ["b6"], "lir")
     cp(T.yb[:, 256:384], B(YB[2], 0, 128), ["b%d" % YB[2]], "yb2")
     store("Y", [(T.osc[4 * k:4 * k + 4, :], T.oqs[32 * k:32 * k + 4, :]) for k in range(4)], hk("oqs", 3))
     for a, b in ((0, 2), (2, 3)):
         store("Y", [(T.y[:, 128 * a:128 * b], T.yb[:, 128 * a:128 * b])], ["yb%d" % c for c in range(a, b)])
-    store("S", [(T.li[1:2, :], T.lir[96:97, :])], ["lir"])
+    store("S", [(T.li[1:2, :], T.lir[0:CH, :])], ["lir"])
 
     issue()
     for q in ("V", "T", "S", "G"):

import numpy as np
from concourse.bass import DstId, RemoteDMATransfer
from concourse.mybir import dt, AluOpType, AxisListType, ActivationFunctionType

F8 = "float8_e4m3fn_x4"
CH = 96
NT = 384
HO = 512
TRI, ONE = 528, 656
ZO, ZC, ZA, ZB, ZT, ZP, NZ = 70, 138, 224, 240, 272, 292, 420
NA = 16
WX = 140 + NA


def sb(n, d):
    return ("sbuf", [128, n], d)


def codes(**names):
    d = {}
    for k, n in names.items():
        d[k], d[k + "s"] = sb(n, F8), sb(n, "uint8")
    return d


F, H, U = "float32", "bfloat16", "uint16"
SCRATCH = {"ps": ("psum", [128, 4096], F)}
SCRATCH.update({k: sb(n, d) for d, names in (
    (H, dict(ub=912, xb=4 * NT, vb=2048, wb=512, eb=520, urb=512, urn=512, q0=128, zb=4 * NZ, k12=24, xw=1024,
             cmp=4 * NT, sg=768, wx=4 * WX, tie=NT + CH, mk=24, hb=512, hx=4 * (CH + NT))),
    (F, dict(kc=48, jj=24, jx=24, ab=48, jbp=1, ip=1, ip1=1, ip2=1, ip3=1, p16f=1, tha=64, tj=12, t8=4, pl=NT, c96=8, c96a=8,
             th8=8, c512=1, nab=1, sc=3, dl=3, mt=NT, x0=48, kl=48, sc0=3, dl0=3, mz=390, scd=3, gd=3, mc=3 * CH, lsb=10,
             lrow=CH, thr=48, hrb=4 * CH, hr0=4 * NT, hr1=4 * CH, yb=NT, lir=1)),
    (U, dict(z16=8, lst1=6, lin=6, off2=24))) for k, n in names.items()})
SCRATCH.update(codes(uq=128, ur1=128, t0=NT + 16, vq=512, wq=128, qe=CH + 512, zq=NZ, cq=NT, wxq=WX, xwq=256,
                     xoq=128, q1=CH, m1=128, big=HO + CH + NT, oq=NT, pe=CH + 128, un=128))
SEMAPHORES = ["sV", "sT", "sS", "sG", "du", "dx0", "dx1", "dx2", "dv0", "dv1", "dv2", "dv3", "dw", "dst",
              "au", "aq", "at", "am", "al", "aa", "go", "go2", "ls"]

OP = AluOpType
AF = ActivationFunctionType
BIG1, BIG16, BIG32 = 1.5 * 2.0 ** 23, 1.5 * 2.0 ** 27, 1.5 * 2.0 ** 28
ULP = 1.03125 * 2.0 ** -24
TINY = 1e-37
FAR = 1e29
C05 = 13421773 * 2.0 ** -28
BANKS = ["b%d" % k for k in range(8)]

ORDER = """
ub xb0 ones ubz jj jx xb1 xb2 ip ip1 q0 wx3 aba tri urb2 nab0 zbz zc1 zc2 zo03 jbp zo12 ip2 urb0 zc0 urb3 urb1 zo11
zo10 uq >au0 t00 z16 t01 zbz2 t02 b1 ur2 ebi eq0 eq3 >at0 >at1 go vb0 kc cmk eq1 zp0 tj zp3 vb1 vb2 vb3 zt4 zo01 ip3
zo00 abb urn un0 zt1 p16f wa zo02 zt7 zt3 zo13 w21 ur1s w20 ur1 zq eq2 b2 b3 sc b0 cm01 b7 cm21 dl zt6 cm20 mt2 cm22
mt1 b6 sg1 sg0 cm10 cm11 cq2 mt0 cm00 zt5 cm12 cq1 cm02 t8 zt2 b2.2 b5 b3.2 b1.2 sc0 dl0 mz1 mz2 sg2 sg3 cq0 b4 b4.2
b4.3 vq0 cm01.2 mz0 kl tha wxa zp1 xz pp zp2 x0 wx2 wx0 wx1 wxx cm20.2 wxq >aa0 >aa1 xs1 zt0 zq2 vq1 b3.3 b2.3 b0.2
b0.3 lst1 b1.3 cm22.2 b6.2 q1 vq2 b7.2 xl2 cm02.2 hr00 b3.4 h60 vq3 >aq0 q1s >aq1 b4.4 >al0 go2 wb xs0 c96 k12 sg4 sg5
hr01 xl1 h50 h70 cm00.2 h71 cm11.2 cm10.2 h61 h51 cm21.2 cq2.2 cm12.2 hr02 cq1.2 pec hrb0 b6.3 hrb2 b1.4 b0.4 hrb1 hb0
b7.3 b2.4 hb1 b4.5 hb2 b0.5 hrb3 hb3 pes h62 pl lrow st0 b1.5 b1.6 b1.7 gd b2.5 b2.6 lsb ls9 b6.4 hr03 m1 cq0.2 b4.6
scd h72 c96a th8 c512 >am0 w22 >am1 mk tie1 tie3 xg0 tie0 h52 b7.4 h73 h53 tie2 h63 wa.2 wq bh6 bh5 b4.7 b5.2 b4.8 b2.7
b3.5 thr1 mc1 xl0 xs2 xg2 mc2 mc0 b1.8 cm11.3 cm12.3 thr2 thr3 cm10.3 b5.3 cm00.3 xg1 b6.5 b3.6 cm02.3 b2.8 b0.6 b0.7
cm01.3 cm03 cq1.3 bh7 cq0.3 thr0 b7.5 xwq hr10 b6.6 b1.9 h10 b4.9 hr11 b0.8 h11 b7.6 b4.10 xo wx2.2 hr12 b5.4 h12 hr13
xoq wx3.2 b3.7 b2.9 h13 wx1.2 wx0.2 bh1 b3.8 off2 wxq.2 b6.7 oq0 st1 oqs0 oqs1 oqs2 b7.7 yb0 oq1 b0.9 oq2 st2 lir st9
yb1 st3 b2.10 yb2 st7 st8
"""


def sched(g, T):
    eng = {"V": g.vector, "T": g.tensor, "S": g.scalar, "G": g, "Y": g.sync}
    cnt = {"V": 0, "T": 0, "S": 0, "G": 0}
    wr, rd, seen, steps, names = {}, {}, {}, [], {}

    def wait(q, reads, writes):
        req = {}
        for k in reads:
            for qq, s, v in wr[k]:
                req[s] = max(req.get(s, 0), v)
            if k in BANKS:
                for qq, s, v in rd.get(k, []):
                    if qq != q:
                        req[s] = max(req.get(s, 0), v)
        for k in writes:
            for qq, s, v in wr.get(k, []) + rd.get(k, []):
                if qq != q or q != "T":
                    req[s] = max(req.get(s, 0), v)
        for s, v in req.items():
            if seen.get((q, s), 0) < v:
                eng[q].wait_ge(T.sem[s], v)
                seen[(q, s)] = v

    def step(q, call, reads, writes, sem=None, val=0):
        k = writes[0]
        names[k] = names.get(k, 0) + 1
        steps.append((k if names[k] == 1 else "%s.%d" % (k, names[k]), q, call, list(reads), list(writes), sem, val))

    def arrive(s, v, keys):
        for k in keys:
            wr[k] = [("far", s, v)]

    def issue():
        by = {s[0]: s for s in steps}
        for name in (ORDER.split() or [s[0] for s in steps]):
            _, q, call, reads, writes, sem, val = by.pop(name)
            wait(q, reads, writes)
            if sem is None:
                cnt[q] += 1
                call(eng[q]).then_inc(T.sem["s" + q], 1)
                mark = (q, "s" + q, cnt[q])
            else:
                call(eng[q])
                mark = ("dma", sem, val)
            for k in reads:
                rd.setdefault(k, []).extend([mark] if sem != "" else [])
            for k in writes:
                wr[k], rd[k] = ([mark] if sem != "" else []), []
        assert not by
    return step, arrive, issue, cnt, steps


def rank_program(g, core, T, topo):
    r = T.rank_of(core)
    if r is None:
        return
    n = len(T.cores)
    nxt, nx2, prv = T.cores[(r + 1) % n], T.cores[(r + 2) % n], T.cores[(r - 1) % n]
    op, arrive, issue, cnt, _ = sched(g, T)
    ps = T.ps
    loc, sent, stores = [0], [], [0]

    def dma(q, pairs, s, v, reads, writes):
        def call(e):
            for o, i in pairs:
                e.dma_start(o, i).then_inc(T.sem[s], 16)
        op(q, call, reads, writes, s, v)

    def store(q, pairs, reads):
        dma(q, pairs, "dst", 0, reads, ["st%d" % stores[0]])
        stores[0] += len(pairs)

    def half(dst, k):
        e = topo.engines(core, dst)
        return e[:len(e) // 2] if k == 0 else e[len(e) // 2:]

    def bits(es):
        return sum(1 << e for e in es)

    def send(dst, out, src, sem, es, reads):
        rid, pid, _ = topo.addr(dst)
        k = ">" + sem + str(len([x for x in sent if x[1:3] == sem]))
        sent.append(k)
        op("G", lambda e: e.remote_dma(out, src, T.sem[sem], T.sem["ls"], pid, rid, bits(es)), reads, [k], "")
        loc[0] += len(es)

    def u8(name, a, b):
        return T[name][:, a:b].bitcast(dt.uint8)

    arrive("au", 8, ["uin"])
    arrive("aq", 32, ["qin"])
    arrive("at", 32, ["bt"])
    arrive("am", 32, ["bm"])
    arrive("al", 8, ["lin"])
    arrive("aa", 16, ["za"])

    def keys(k):
        return [k] if isinstance(k, str) else k

    def V(f, reads, writes):
        op("V", f, reads, keys(writes))

    def S(f, reads, writes):
        op("S", f, reads, keys(writes))

    def G(f, reads, writes):
        op("G", f, reads, keys(writes))

    def memset(ap, c, key, after=()):
        V(lambda e: e.memset(ap, c), list(after), key)

    def iota(ap, pattern, key, cm=0, base=0, after=()):
        G(lambda e: e.iota(ap, pattern, base, cm, allow_small_or_imprecise_dtypes=True), list(after), key)

    def asel(out, in_, pattern, o, fill, base, cm, reads, key):
        G(lambda e: e.affine_select(out, in_, pattern, o, fill, base, cm), reads, key)

    def ts(out, in0, s1, o, reads, key):
        V(lambda e: e.tensor_scalar(out, in0, s1, None, o), reads, key)

    def ts2(out, in0, s1, o1, s2, o2, reads, key):
        V(lambda e: e.tensor_scalar(out, in0, s1, s2, o1, o2), reads, key)

    def tt(out, in0, in1, o, reads, key):
        V(lambda e: e.tensor_tensor(out, in0, in1, o), reads, key)

    def cp(out, in_, reads, key):
        V(lambda e: e.tensor_copy(out, in_), reads, key)

    def act(out, in_, f, bias, scale, reads, key):
        S(lambda e: e.activation(out, in_, f, bias=bias, scale=scale), reads, key)

    def zeros(w):
        return T.ub[:, 8:8 + w]

    def ones(w):
        return T.ub[:, ONE:ONE + w]

    def quant(out, a, b, src, reads, key):
        V(lambda e: e.quantize_mx(T[out][:, a:b], T[out + "s"][:, a:b], src), reads, key)

    def mm(bank, w, L, l0, R, r0, start, stop, reads):
        op("T", lambda e: e.matmul_mx(ps[:, 512 * bank:512 * bank + w], T[L][:, l0:l0 + 128], T[L + "s"][:, l0:l0 + 128],
                                      T[R][:, r0:r0 + w], T[R + "s"][:, r0:r0 + w], start, stop), reads, ["b%d" % bank])

    def B(bank, a, b, s=1):
        return ps[:, 512 * bank + a:512 * bank + b:s]

    def pick_c(dst, d0, w, src, a, b, off, o0, reads, key):
        V(lambda e: e.tensor_copy(T[dst][:, d0:d0 + w].bitcast(dt.uint32),
                                  T[src][:, a:b].bitcast(dt.uint32).indirect(T[off][:, o0:o0 + w // 16])), reads, key)

    def pick_s(dst, d0, w, src, a, b, off, o0, reads, key):
        S(lambda e: e.activation(T[dst + "s"][:, d0:d0 + w], T[src + "s"][:, a:b].indirect(T[off][:, o0:o0 + w // 16]),
                                 AF.Copy), reads, key)

    def hk(key, k=4):
        return [key + str(i) for i in range(k)]

    pp = T.hb[:, 4 * CH:512]
    wa = T.xw[:, 515:1024:4]

    dma("Y", [(T.ub[:, 0:8], T.u[:, 0:8])], "du", 16, [], ["ub"])
    for c in range(3):
        dma("Y", [(T.xb[:, 512 * c:512 * c + 512], T.x[:, 512 * c:512 * c + 512])], "dx%d" % c, 16, [], ["xb%d" % c])

    memset(T.ub[:, 8:TRI], 0.0, "ubz")
    memset(ones(256), 1.0, "ones")
    iota(T.jj[:], [[0, 6], [128, 4]], "jj", 1)
    iota(T.ip[:], [[0, 1]], "ip", 2)
    iota(T.q0[:], [[0, 8], [1, 16]], "q0")
    memset(T.z16[:], 0, "z16")
    memset(T.zb[:, 0:4 * ZA], 0.0, "zbz")
    quant("uq", 0, 128, T.ub[:, 0:512], ["ub", "ubz"], "uq")
    rid, pid, _ = topo.addr(prv)
    e0 = half(prv, 0)
    op("G", lambda e: e.remote_dma_fused(
        [RemoteDMATransfer(dst_ids=[DstId(rid=rid, pnc=pid)], dma_engine_mask=bits(e0[:4]), remote_sem=T.sem["au"],
                           src=u8("uq", 0, 2), dst=u8("t0", NT, NT + 2)),
         RemoteDMATransfer(dst_ids=[DstId(rid=rid, pnc=pid)], dma_engine_mask=bits(e0[4:]), remote_sem=T.sem["au"],
                           src=T.uqs[:, 0:8], dst=T.t0s[:, NT:NT + 8])], local_sem=T.sem["ls"]), ["uq"], [">au0"], "")
    loc[0] += len(e0)
    asel(T.eb[:], zeros(520), [[-1, 130], [1000, 4]], OP.not_equal, 1.0, 1, 1, ["ubz"], "ebi")
    asel(T.ub[:, TRI:ONE], ones(128), [[1, 128]], OP.is_gt, 0.0, 0, -1, ["ones"], "tri")
    iota(T.kc[:], [[0, 2], [16, 6], [0, 4]], "kc")
    iota(T.tha[:], [[0, 8], [1000, 2], [0, 4]], "tha", 0, CH - 8)
    act(T.jx[:], T.jj[:], AF.Identity, BIG32, 1.0, ["jj"], "jx")
    act(T.ip1[:], T.ip[:], AF.Identity, -15.0, 1.0, ["ip"], "ip1")
    act(T.ab[:, 0:24], T.jx[:], AF.Identity, -BIG32, 1.0, ["jx"], "aba")
    act(T.ip2[:], T.ip1[:], AF.Identity, BIG1, 1.0 / 32, ["ip1"], "ip2")
    act(T.jbp[:], T.ab[:, 0:1], AF.Identity, T.jj[:, 0:1], -1.0, ["aba", "jj"], "jbp")
    act(T.ip3[:], T.ip2[:], AF.Identity, -BIG1, 1.0, ["ip2"], "ip3")
    act(T.ab[:, 24:48], zeros(24), AF.Identity, T.jbp[:, 0:1], 1.0, ["ubz", "jbp"], "abb")
    asel(T.cmp[:, 3:4 * NT:4], zeros(NT), [[0, NT]], OP.not_equal, -7.5, 0, 1, ["ubz"], ["cmk", "cm03"])
    act(T.p16f[:], T.ip3[:], AF.Identity, T.jj[:, 0:1], -16.0, ["ip3", "jj"], "p16f")
    act(T.wx[:, 51:560:4], zeros(128), AF.Copy, 0.0, 1.0, ["ubz"], "wx3")
    for t in range(4):
        for a in range(2):
            k = 17 if t < 3 else 16
            b = (8, 4 * ZO + 4)[a]
            act(T.zb[:, b + t:b + 16 * k:16], ones(k), AF.Copy, 0.0, 1.0, ["ones", "zbz"], "zo%d%d" % (a, t))
    for t in range(3):
        act(T.zb[:, 4 * ZC + 4 + t:4 * ZC + 192:8], ones(24), AF.Copy, 0.0, 1.0, ["ones", "zbz"], "zc%d" % t)
    for t in range(4):
        act(T.urb[:, t:512:4], zeros(128), AF.Identity, T.ub[:, t:t + 1], 1.0, ["ub", "ubz"], "urb%d" % t)
    act(wa, T.q0[:], AF.Abs, T.p16f[:, 0:1], -1.0, ["q0", "p16f"], "wa")

    for c in range(3):
        quant("t0", 128 * c, 128 * c + 128, T.xb[:, 512 * c:512 * c + 512], ["xb%d" % c], "t0%d" % c)
    for b in range(4):
        quant("qe", CH + 128 * b, CH + 128 * b + 128, T.eb[:, 4 - b:516 - b], ["ebi"], "eq%d" % b)
    t0 = hk("t0", 3)
    send(nx2, u8("big", CH, CH + NT), u8("t0", 0, NT), "at", topo.engines(core, nx2), t0)
    send(nx2, T.bigs[:, CH:CH + NT], T.t0s[:, 0:NT], "at", topo.engines(core, nx2), t0)
    op("G", lambda e: e.sem_inc(T.sem["go"], 1), [">at0", ">at1"], ["go"], "go", 1)
    for i in range(4):
        dma("Y", [(T.vb[:, 512 * i:512 * i + 512], T.v[:, 512 * i:512 * i + 512])], "dv%d" % i, 16, ["go", "uin"], ["vb%d" % i])
    iota(T.tj[:], [[-128, 3], [128, 4]], "tj")
    iota(T.t8[:], [[8, 4]], "t8", 0, -12)
    iota(T.xw[:, 0:512], [[0, 512]], "xz")
    iota(pp, [[1, 128]], "pp")
    iota(T.xw[0:32, 1:96:4], [[16, 24]], "xs0", 0, -192, ["xz"])
    memset(T.xw[32:64, 1:96:4], 192.0 + CH, "xs1", ["xz"])
    iota(T.c96[:], [[0, 8]], "c96", 0, CH)
    iota(T.k12[:], [[1, 24]], "k12", 0, -12)
    asel(T.c96a[:], T.c96[:], [[-16, 8]], OP.is_ge, 0.0, 0, 1, ["c96"], "c96a")
    asel(T.c512[:], zeros(1), [[1, 1]], OP.is_ge, float(HO), -CH, 1, ["ubz"], "c512")
    asel(T.th8[:], T.c96a[:], [[16, 8]], OP.is_ge, 0.0, 15, -1, ["c96a"], "th8")
    iota(T.pl[:], [[1, NT]], "pl")
    memset(T.zb[:, 4 * ZB:4 * NZ], 0.0, "zbz2")
    for t in range(3):
        iota(T.zb[0:CH, 4 * ZP + 65 * t:4 * ZP + 64 * t + 64:8], [[0, 8]], "zp%d" % t, 0, 1, ["zbz2"])
    iota(T.zb[0:CH, 4 * ZP + 7:4 * ZP + 192:8], [[0, 24]], "zp3", 0, 1, ["zbz2"])
    quant("zq", 0, ZA, T.zb[:, 0:4 * ZA], ["zbz"] + hk("zo0") + hk("zo1") + hk("zc", 3), "zq")
    quant("pe", CH, CH + 128, T.urb[:], hk("urb"), "ur2")
    act(T.urn[:], T.urb[:], AF.Copy, 0.0, -1.0, hk("urb"), "urn")
    quant("un", 0, 128, T.urn[:], ["urn"], "un0")

    ROW = (0, 6, 7)
    SC = 126

    def slot(c, t, w=128):
        return T.cmp[:, 512 * c + t:512 * c + 4 * w:4]

    def against(c, t):
        if c == t:
            tt(slot(c, c), B(ROW[c], 0, 128), T.mt[:, 128 * c:128 * c + 128], OP.is_lt, ["b%d" % ROW[c], "mt%d" % c], "cm%d%d" % (c, c))
        else:
            ts(slot(c, t), B(ROW[c], 0, 128), T.sc[:, t:t + 1], OP.is_le if t < c else OP.is_lt, ["b%d" % ROW[c], "sc"], "cm%d%d" % (c, t))

    def sign(c, t):
        act(T.sg[:, 128 * c:128 * c + 128], B(ROW[c], 0, 128), AF.Sign, T.sc[:, t:t + 1], -1.0, ["b%d" % ROW[c], "sc"], "sg%d" % c)

    def relu(c, t, k):
        act(slot(c, t), T.sg[:, 128 * k:128 * k + 128], AF.Relu, 0.0, 1.0, ["sg%d" % k], "cm%d%d" % (c, t))

    def score(sc, dl, at):
        cols = ps[:, 512 + at:2048:512]
        act(T[sc][:], cols, AF.Copy, 0.0, 1.0, ["b1", "b2", "b3"], sc)
        act(T[dl][:], cols, AF.Abs, TINY, ULP, ["b1", "b2", "b3"], dl)

    def shift(c):
        act(T.mt[:, 128 * c:128 * c + 128], T.ub[:, TRI:ONE], AF.Identity, T.sc[:, c:c + 1], T.dl[:, c:c + 1], ["tri", "sc", "dl"], "mt%d" % c)

    def pack(c, more=()):
        quant("cq", 128 * c, 128 * c + 128, T.cmp[:, 512 * c:512 * c + 512], hk("cm%d" % c, 3) + ["cmk"] + list(more), "cq%d" % c)

    def position(c):
        mm(4, 128, "cq", 128 * c, "zq", (2, ZO, 0)[c], c == 2, c == 0, ["cq%d" % c, "zq"])

    def Rm(i, bank, q, q0, w, keys):
        mm(bank, w, "vq", 128 * i, q, q0, True, True, keys + ["vq%d" % i])

    def Ra(i, bank, out, w2):
        act(T[out][:, w2 * i:w2 * i + w2], B(bank, 0, w2), AF.Relu, 0.0, C05, ["b%d" % bank], out + str(i))

    def D(i, bank, q, q0, w, keys):
        mm(bank, w, "qe", CH + 128 * i, q, q0, True, True, keys + ["eq%d" % i])

    def add(i, bank, h, c0, w, hr, key):
        tt(T[h][:, 4 * c0 + i:4 * (c0 + w):4], T[hr][:, w * i:w * i + w], B(bank, 0, w), OP.add, [hr + str(i), "b%d" % bank], key + str(i))

    def D0(i, bank):
        D(i, bank, "big", CH, NT, ["bt"])

    def R0(i, bank):
        Rm(i, bank, "big", CH, NT, ["bt"])
        Ra(i, bank, "hr0", NT)

    def A0(i, bank):
        for c in range(3):
            a = 4 * (CH + 128 * c)
            tt(T.hx[:, a + i:a + 512:4], T.hr0[:, NT * i + 128 * c:NT * i + 128 * c + 128], B(bank, 128 * c, 128 * c + 128),
               OP.add, ["hr0%d" % i, "b%d" % bank], "h%d%d" % (c + 5, i))

    for c in range(3):
        mm(1 + c, 128, "t0", 128 * c, "t0", NT - SC, True, True, ["t0%d" % c, "t02", "uin"])
    pick_s("ur1", 0, 128, "t0", NT, NT + 2, "z16", 0, ["uin", "z16"], "ur1s")
    pick_c("ur1", 0, 128, "t0", NT, NT + 2, "z16", 0, ["uin", "z16"], "ur1")
    for c in (2, 0, 1):
        mm(ROW[c], 128, "ur1", 0, "t0", 128 * c, True, True, ["t0%d" % c, "ur1", "ur1s"])
    score("sc", "dl", SC), shift(2), sign(0, 2), sign(1, 2), shift(1), shift(0), relu(1, 2, 1), relu(0, 2, 0)
    for c, t in ((2, 0), (2, 1), (2, 2), (0, 1), (1, 0), (1, 1)):
        against(c, t)
    pack(2), against(0, 0), pack(1), pack(0)
    position(2), position(1), position(0)
    for c in range(3):
        mm(1 + c, 128, "big", CH + 128 * c, "pe", CH, True, True, ["bt", "ur2"])
    mm(5, NT, "pe", CH, "big", CH, True, True, ["bt", "ur2"])
    zt = 4 * ZT
    act(T.zb[:, zt:zt + 12], T.tj[:], AF.Identity, T.ab[:, 0:1], 1.0, ["tj", "aba", "zbz2"], "zt0")
    act(T.zb[:, zt + 12:zt + 16], T.ab[:, 24:28], AF.Copy, 0.0, 1.0, ["abb", "zbz2"], "zt1")
    act(T.zb[:, zt + 16:zt + 20], T.t8[:], AF.Identity, T.ip3[:, 0:1], 1.0, ["t8", "ip3", "zbz2"], "zt2")
    act(T.zb[:, zt + 20:zt + 24], zeros(4), AF.Identity, T.p16f[:, 0:1], 1.0, ["ubz", "p16f", "zbz2"], "zt3")
    act(T.zb[:, zt + 24:zt + 28], T.ab[:, 0:4], AF.Copy, 0.0, -1.0 / HO, ["aba", "zbz2"], "zt4")
    act(T.zb[:, zt + 28:zt + 32], T.ab[:, 24:28], AF.Copy, 0.0, -1.0, ["abb", "zbz2"], "zt5")
    act(T.zb[:, zt + 32:zt + 36], T.ab[:, 0:4], AF.Copy, 0.0, 1.0, ["aba", "zbz2"], "zt6")
    act(T.zb[:, zt + 40:zt + 52], T.ab[:, 24:36], AF.Copy, 0.0, 1.0, ["abb", "zbz2"], "zt7")
    act(T.xw[:, 512:1024:4], wa, AF.Relu, float(HO), -float(HO), ["wa"], "w20")
    act(T.xw[:, 513:1024:4], wa, AF.Relu, 0.5, -0.5, ["wa"], "w21")
    act(T.nab[:], T.ab[:, 0:1], AF.Identity, -CH / HO, 1.0 / HO, ["aba"], "nab0")
    act(T.xw[:, 488:491], T.ab[:, 0:3], AF.Copy, 0.0, 1.0, ["aba", "xz"], "xl1")
    act(T.xw[:, 480:483], T.ab[:, 24:27], AF.Copy, 0.0, 1.0, ["abb", "xz"], "xl2")
    act(T.xw[64:96, 1:96:4], T.ub[64:96, 8:32], AF.Identity, T.p16f[64:96, 0:1], 1.0, ["ubz", "p16f", "xz"], "xs2")
    score("sc0", "dl0", 0)
    for c in range(3):
        act(T.mz[:, 130 * c:130 * c + 129], T.ub[:, TRI:ONE + 1], AF.Identity, T.sc0[:, c:c + 1], T.dl0[:, c:c + 1],
            ["tri", "ones", "sc0", "dl0"], "mz%d" % c)
    tt(T.wx[:, 560:560 + 4 * NA], T.tha[:], B(4, 0, 4 * NA), OP.is_le, ["tha", "b4"], "wxa")
    ts2(T.kl[:], B(4, 0, 48), BIG16, OP.add, BIG16, OP.subtract, ["b4"], "kl")
    tt(T.x0[:], T.kl[:], T.kc[:], OP.is_equal, ["kl", "kc"], "x0")
    for t in range(3):
        ts2(T.wx[:, 48 + t:560:4], T.q0[:], T.kl[:, t:t + 1], OP.add, B(4, 64 + t, 65 + t), OP.is_equal, ["q0", "b4", "kl"], "wx%d" % t)
    tt(T.wx[:, 0:48], T.x0[:], T.ab[:], OP.mult, ["x0", "aba", "abb"], "wxx")
    quant("wxq", 0, WX, T.wx[:], hk("wx") + ["wxx", "wxa"], ["wxq", "wxqa"])
    mm(0, 128, "wxq", 12, "wxq", 0, True, False, ["wxq"])
    mm(0, 128, "wxq", 12, "wxq", 6, False, True, ["wxq"])
    D0(0, 1), D0(1, 2)
    quant("zq", ZB, NZ, T.zb[:, 4 * ZB:4 * NZ], ["zbz2"] + hk("zp") + hk("zt", 8), "zq2")
    cp(T.lst1[:], B(0, 0, 6), ["b0"], "lst1")
    send(nx2, u8("zq", ZA, ZA + NA), u8("wxq", 140, WX), "aa", half(nx2, 1), ["wxqa"])
    send(nx2, T.zqs[:, ZA:ZA + NA], T.wxqs[:, 140:WX], "aa", half(nx2, 0), ["wxqa"])
    pick_s("q1", 0, CH, "t0", 0, NT, "lst1", 0, t0 + ["lst1"], "q1s")
    pick_c("q1", 0, CH, "t0", 0, NT, "lst1", 0, t0 + ["lst1"], "q1")
    send(nxt, u8("qe", 0, CH), u8("q1", 0, CH), "aq", topo.engines(core, nxt), ["q1"])
    send(nxt, T.qes[:, 0:CH], T.q1s[:, 0:CH], "aq", topo.engines(core, nxt), ["q1s"])
    send(nx2, T.lin[:], T.lst1[:], "al", half(nx2, 1), ["lst1"])
    op("G", lambda e: e.sem_inc(T.sem["go2"], 1), [">aq0", ">aq1"], ["go2"], "go2", 1)
    dma("Y", [(T.wb[:], T.w[:])], "dw", 16, ["go2", "qin"], ["wb"])
    for i in range(4):
        quant("vq", 128 * i, 128 * i + 128, T.vb[:, 512 * i:512 * i + 512], ["vb%d" % i], "vq%d" % i)

    for c in (1, 2):
        ts(slot(c, 0), B(5, 128 * c, 128 * c + 128), T.sc0[:, 0:1], OP.is_le, ["b5", "sc0"], "cm%d0" % c)
    for k, (c, t) in ((2, (0, 1)), (3, (0, 2)), (4, (1, 2)), (5, (2, 1))):
        bias = T.mz[:, 130 * t + 128:130 * t + 129] if t < c else T.sc0[:, t:t + 1]
        act(T.sg[:, 128 * k:128 * k + 128], B(5, 128 * c, 128 * c + 128), AF.Sign, bias, -1.0, ["b5", "sc0", "mz%d" % t], "sg%d" % k)
        relu(c, t, k)
    R0(0, 3), R0(1, 6), R0(2, 7)
    for c in range(3):
        tt(slot(c, c), B(5, 128 * c, 128 * c + 128), T.mz[:, 130 * c:130 * c + 128], OP.is_lt, ["b5", "mz%d" % c], "cm%d%d" % (c, c))
    pack(0), pack(1), pack(2)
    D0(2, 3)
    A0(0, 1), A0(1, 2), A0(2, 3)

    RB, DB = (4, 0, 6, 7), (1, 2, 4, 0)
    for i in range(4):
        Rm(i, RB[i], "qe", 0, 128, ["qin", "eq0"])
        Ra(i, RB[i], "hrb", CH)
    for i in range(4):
        D(i, DB[i], "qe", 0, 128, ["qin", "eq0"])
    for i in range(4):
        add(i, DB[i], "hb", 0, CH, "hrb", "hb")
    quant("m1", 0, 128, T.hb[:], ["pp"] + hk("hb"), "m1")
    send(nxt, u8("big", 0, CH), u8("m1", 0, CH), "am", topo.engines(core, nxt), ["m1"])
    send(nxt, T.bigs[:, 0:CH], T.m1s[:, 0:CH], "am", topo.engines(core, nxt), ["m1"])

    zk = ["zq", "zq2", "za"]
    ek = hk("eq", 3) + ["lin"]
    pick_s("pe", 0, CH, "qe", CH, CH + NT, "lin", 0, ek, "pes")
    pick_c("pe", 0, CH, "qe", CH, CH + NT, "lin", 0, ek, "pec")
    act(T.lrow[:], T.pl[:].indirect(T.lin[:]), AF.Copy, 0.0, 1.0, ["pl", "lin"], "lrow")
    R0(3, 6), D0(3, 7)
    for t in range(3):
        mm(1, 128, "qe", CH + 128 * t, "zq", ZA - 16 * t, t == 0, t == 2, zk + ["eq%d" % t])
    mm(2, 128, "pe", 0, "zq", ZA, True, False, zk + ["pes", "pec", "ur2"])
    mm(2, 128, "pe", 0, "zq", ZA + 10, False, True, zk + ["pes", "pec", "ur2"])
    for c in range(3):
        mm(4, 128, "cq", 128 * c, "zq", ZA - 16 * c, c == 0, False, zk + ["cq%d" % c])
    act(T.lsb[:, 0:9], B(2, ZT - ZA, ZT - ZA + 9), AF.Copy, 0.0, 1.0, ["b2"], "lsb")
    act(T.gd[:], B(1, 0, 48, 16), AF.Identity, -FAR, FAR, ["b1"], "gd")
    quant("wq", 0, 128, T.wb[:], ["wb"], "wq")
    A0(3, 7)

    def L(i):
        return T.lsb[:, i:i + 1]
    tt(T.scd[:], T.sc0[:], T.gd[:], OP.add, ["sc0", "gd"], "scd")
    ts(T.mk[:], T.k12[:], L(4), OP.is_equal, ["k12", "lsb"], "mk")
    for t in range(3):
        ts2(T.tie[:, 128 * t:128 * t + 128], pp, L(t), OP.is_gt, TINY, OP.mult, ["pp", "lsb"], "tie%d" % t)
    ts2(T.xw[:, 514:1024:4], T.q0[:], L(5), OP.is_equal, T.c512[:, 0:1], OP.mult, ["q0", "lsb", "c512"], "w22")
    ts(wa, T.q0[:], L(5), OP.is_equal, ["q0", "lsb"], "wa")
    act(T.lsb[:, 9:10], L(6), AF.Identity, T.nab[:, 0:1], 1.0, ["lsb", "nab0"], "ls9")
    ts2(T.tie[:, NT:NT + CH], T.lrow[:], L(0), OP.is_gt, TINY, OP.mult, ["lrow", "lsb"], "tie3")
    for t in range(3):
        act(T.mc[:, CH * t:CH * t + CH], T.ub[:, TRI - 128 * t:TRI - 128 * t + NT].indirect(T.lin[:]), AF.Identity,
            T.scd[:, t:t + 1], T.dl0[:, t:t + 1], ["ubz", "tri", "ones", "lin", "scd", "dl0"], "mc%d" % t)
    for i, (at, c) in enumerate(((98, T.lsb[0:CH, 9:10]), (99, T.lsb[0:CH, 7:8]), (3, T.jbp[0:CH, 0:1]))):
        act(T.xw[0:CH, at:at + 96:4], T.mk[0:CH, :], AF.Copy, 0.0, c, ["mk", "lsb", "ls9", "jbp", "xz"], "xg%d" % i)
    act(T.xw[0:CH, 483:492:8], T.lsb[0:CH, 3:9:5], AF.Copy, 0.0, 1.0, ["lsb", "xz"], "xl0")
    act(T.thr[:, 1:48:2], T.mk[:], AF.Copy, 0.0, float(CH), ["mk"], "thr3")
    for t in range(3):
        act(T.thr[:, 16 * t:16 * t + 16:2], T.th8[:], AF.Identity, T.gd[:, t:t + 1], 1.0, ["th8", "gd"], "thr%d" % t)
    AB = (5, 2, 3)
    for t in range(3):
        mm(AB[t], 128, "pe", CH, "big", CH + 128 * t, True, False, ["bt", "ur2"])
    store("Y", [(T.li[0:1, :], T.lrow[0:1, :])], ["lrow"])
    for c in range(3):
        a = CH + 128 * c
        quant("big", HO + a, HO + a + 128, T.hx[:, 4 * a:4 * a + 512], hk("h%d" % (c + 5)), "bh%d" % (c + 5))
    quant("xwq", 0, 256, T.xw[:], ["xz", "w20", "w21", "w22", "wa"] + hk("xg", 3) + hk("xl", 3) + hk("xs", 3), "xwq")

    mk = ["bt", "bm"]
    mm(1, 128, "pe", CH, "big", 0, True, True, mk + ["ur2"])
    for t in range(3):
        mm(AB[t], 128, "big", 0, "un", 0, False, True, mk + ["un0"])
    mm(0, 128, "pe", CH, "big", 0, True, False, mk + ["ur2"])
    mm(0, 128, "big", 0, "un", 0, False, True, mk + ["un0"])
    RN, DN = (6, 7, 6, 7), (1, 0, 5, 2)
    for i in range(4):
        Rm(i, RN[i], "big", 0, 128, mk)
        Ra(i, RN[i], "hr1", CH)
    for t in range(3):
        tt(slot(1, t, CH), B(1, 0, CH), T.mc[:, CH * t:CH * t + CH], OP.is_lt, ["b1", "mc%d" % t], "cm1%d" % t)
    pack(1)
    mm(4, 128, "cq", 128, "zq", ZC, False, False, zk + ["cq1"])
    for t in range(3):
        tt(slot(0, t), B(AB[t], 0, 128), T.tie[:, 128 * t:128 * t + 128], OP.is_lt, ["b%d" % AB[t], "tie%d" % t], "cm0%d" % t)
    tt(slot(0, 3, CH), B(0, 0, CH), T.tie[:, NT:NT + CH], OP.is_lt, ["b0", "tie3"], "cm03")
    for i in range(4):
        D(i, DN[i], "big", 0, 128, mk)
    pack(0, ["cm03"])
    mm(4, 128, "cq", 0, "zq", ZP, False, True, zk + ["cq0"])
    mm(3, 128, "xwq", 128, "xwq", 24, True, False, ["xwq"])
    for i in range(4):
        add(i, DN[i], "hx", 0, CH, "hr1", "h1")
    tt(T.xw[:, 0:96:2], B(4, 0, 48), T.thr[:], OP.is_lt, hk("thr") + ["b4", "xwq"], "xo")
    for t in range(4):
        s, a = (T.gd[:, t:t + 1], 16 * t) if t < 3 else (0.0, 1)
        ts2(T.wx[:, 48 + t:560:4], pp, s, OP.add, B(4, a, a + 1), OP.is_equal, ["pp", "gd", "b4"], "wx%d" % t)
    quant("xoq", 0, 128, T.xw[:, 0:512], ["xo", "xwq"], "xoq")
    mm(3, 128, "xwq", 128, "xoq", 0, False, True, ["xoq", "xwq"])
    quant("big", HO, HO + 128, T.hx[:, 0:512], hk("h5") + hk("h1") + ["bh5"], "bh1")
    cp(T.off2[:], B(3, 0, 24), ["b3"], "off2")
    quant("wxq", 12, 140, T.wx[:, 48:560], hk("wx"), "wxq")
    mm(6, 128, "wxq", 12, "xwq", 0, True, True, ["wxq", "xwq"])
    al = ["bh5", "bh6", "bh7", "bh1", "off2"] + mk
    YB = (7, 0, 2)
    for c in range(3):
        pick_s("oq", 128 * c, 128, "big", 0, HO + CH + NT, "off2", 8 * c, al, "oqs%d" % c)
        pick_c("oq", 128 * c, 128, "big", 0, HO + CH + NT, "off2", 8 * c, al, "oq%d" % c)
        mm(YB[c], 128, "wq", 0, "oq", 128 * c, True, True, ["wq", "oq%d" % c, "oqs%d" % c])
        if c != 1:
            a = max(128 * c - 128, 0)
            store("Y", [(T.oc[:, 4 * a:512 * c + 512], u8("oq", a, 128 * c + 128))], ["oq1", "oq2"] if c else ["oq0"])
    for c in range(2):
        act(T.yb[:, 128 * c:128 * c + 128], B(YB[c], 0, 128), AF.Copy, 0.0, 1.0, ["b%d" % YB[c]], "yb%d" % c)
    ts(T.lir[:], B(6, 120, 121), B(6, 122, 123), OP.add, ["b6"], "lir")
    cp(T.yb[:, 256:384], B(YB[2], 0, 128), ["b%d" % YB[2]], "yb2")
    store("Y", [(T.osc[4 * k:4 * k + 4, :], T.oqs[32 * k:32 * k + 4, :]) for k in range(4)], hk("oqs", 3))
    for a, b in ((0, 2), (2, 3)):
        store("Y", [(T.y[:, 128 * a:128 * b], T.yb[:, 128 * a:128 * b])], ["yb%d" % c for c in range(a, b)])
    store("S", [(T.li[1:2, :], T.lir[0:CH, :])], ["lir"])

    issue()
    for q in ("V", "T", "S", "G"):
        g.wait_ge(T.sem["s" + q], cnt[q])
    g.wait_ge(T.sem["ls"], loc[0])
    g.wait_ge(T.sem["dst"], 16 * stores[0])
